import numpy as np
import ml_dtypes


def mxq(x, axis, fmt="e4m3"):
    dtype, down = {"e4m3": (ml_dtypes.float8_e4m3fn, 7), "e5m2": (ml_dtypes.float8_e5m2, 14)}[fmt]
    v = np.moveaxis(np.asarray(x, np.float32).astype(ml_dtypes.bfloat16).astype(np.float64), axis, -1)
    blocks = v.reshape(v.shape[:-1] + (-1, 32))
    amax = np.abs(blocks).max(-1, keepdims=True)
    byte = np.maximum(np.where(amax > 0, np.frexp(amax)[1] - 1 + 127, 0) - down, 1)
    scale = np.exp2(byte - 127.0)
    codes = (blocks / scale).astype(np.float32).astype(dtype).astype(np.float64)
    return np.moveaxis((codes * scale).reshape(v.shape), -1, axis)


WIDE = False


def mx_kscale(k):
    if not WIDE:
        return np.ones(k)
    levels = np.array([10, -10, 5, -5, 0])
    if k % 512:
        return np.exp2(np.random.permutation(np.resize(levels, k // 32))).repeat(32)
    a = np.empty((k // 512, 16))
    for p in range(k // 512):
        a[p, :8] = np.random.permutation(np.resize(levels, 8))
        for g in range(8):
            far = levels[np.abs(levels - a[p, g]) >= 10]
            a[p, g + 8] = far[np.random.randint(len(far))]
    return np.exp2(a.ravel()).repeat(32)


def f64(x):
    return np.asarray(x).astype(np.float64)


def striped(idx):
    return np.tile(idx.reshape(-1, 16).T, (8, 1)).astype(np.uint16)


def unstriped(offs):
    return offs[:16].T.reshape(-1).astype(np.int64)


E2M1 = np.array([0.0, 0.5, 1.0, 1.5, 2.0, 3.0, 4.0, 6.0, -0.0, -0.5, -1.0, -1.5, -2.0, -3.0, -4.0, -6.0])


def pack_weight(w, fmt):
    k, n = w.shape
    w = f64(np.asarray(w, np.float32).astype(ml_dtypes.bfloat16)).reshape(k // 32, 32, n)
    amax = np.abs(w).max(1)
    if fmt == "e4m3":
        byte = np.frexp(amax)[1] - 1 + 127 - 7
    else:
        mant, ex = np.frexp(amax / 6.0)
        byte = np.where(mant > 0.5, ex, ex - 1) + 127
    byte = np.clip(np.where(amax > 0, byte, 1), 1, 254)
    scaled = (w * np.exp2(127.0 - byte)[:, None, :]).reshape(k, n).astype(np.float32)
    by_word = np.ascontiguousarray(scaled.reshape(k // 512, 128, 4, n).transpose(0, 1, 3, 2))
    if fmt == "e4m3":
        words = by_word.astype(ml_dtypes.float8_e4m3fn).view(np.uint8)
    else:
        c = by_word.astype(ml_dtypes.float4_e2m1fn).view(np.uint8) & 0xF
        words = (c[..., 0::2] | (c[..., 1::2] << 4)).reshape(k // 512, 128, 2 * n)
    return np.ascontiguousarray(words), np.ascontiguousarray(byte.astype(np.uint8).reshape(k // 512, 16, n))


def unpack_weight(words, scales, fmt):
    g, _, n = scales.shape
    words = np.ascontiguousarray(words).reshape(g, 128, n, -1)
    if fmt == "e4m3":
        vals = words.view(ml_dtypes.float8_e4m3fn).astype(np.float64)
    else:
        nib = np.empty((g, 128, n, 4), np.uint8)
        nib[..., 0::2] = words & 0xF
        nib[..., 1::2] = words >> 4
        vals = E2M1[nib]
    vals = vals * np.repeat(np.exp2(scales.astype(np.float64) - 127.0), 8, axis=1)[..., None]
    return vals.transpose(0, 1, 3, 2).reshape(g * 512, n)


K, T, E, C, N = 1536, 1536, 12, 256, 128


def by_expert(wq, xq):
    return np.concatenate([wq[e].T @ xq[:, e * C:(e + 1) * C] for e in range(E)], axis=1)


def setup_inputs():
    n = np.random.standard_normal
    s = mx_kscale(K)[:, None]
    first = np.random.permutation(np.repeat(np.arange(E), T // E))
    second = (first + 1 + np.random.permutation(np.repeat(np.arange(E - 1), -(-T // (E - 1)))[:T])) % E
    while np.bincount(second, minlength=E).max() != T // E:
        load = np.bincount(second, minlength=E); hi, lo = int(load.argmax()), int(load.argmin())
        t = np.flatnonzero((second == hi) & (first != lo))[0]; second[t] = lo
    slot_token = np.empty(E * C, np.int64); pos = np.empty((2, T), np.int64); fill = np.zeros(E, np.int64)
    place = np.stack([np.random.permutation(C) for _ in range(E)])
    for r, deal in enumerate((first, second)):
        for t in np.random.permutation(T):
            e = deal[t]; j = e * C + place[e, fill[e]]; fill[e] += 1; slot_token[j] = t; pos[r, t] = j
    g = np.random.uniform(0.2, 0.8, T)
    x = pack_weight(n((K, T)) * s, "e4m3")
    return {
        "x_words": x[0],
        "x_scales": x[1],
        "w": (n((E + 1, K, N)) / np.sqrt(K) / s[None]).astype(np.float32),
        "b": (0.3 * n((N, E + 1))).astype(np.float32),
        "gate": np.stack([np.tile(g, (N, 1)), np.tile(1.0 - g, (N, 1))]).astype(np.float32),
        "offs": striped(slot_token),
        "pos1": striped(pos[0]),
        "pos2": striped(pos[1]),
    }


def reference(x_words, x_scales, w, b, gate, offs, pos1, pos2):
    idx = unstriped(offs)
    wq = mxq(f64(w), 1, "e4m3")
    xs = unpack_weight(x_words, x_scales, "e4m3")
    ys = (wq[E].T @ xs) + f64(b)[:, E:]
    xq = unpack_weight(x_words, x_scales, "e4m3")[:, idx]
    y = by_expert(wq, xq)
    y = y + np.repeat(f64(b)[:, :E], C, axis=1)
    return ys + f64(gate[0]) * y[:, unstriped(pos1)] + f64(gate[1]) * y[:, unstriped(pos2)]

@@ -1,0 +1,224 @@
+from contextlib import ExitStack
+
+import concourse.mybir as mybir
+from concourse.masks import make_identity
+
+K, T, E, C, N = 1536, 1536, 12, 256, 128
+S = E * C
+FLOPS = 2 * K * N * (S + T)
+
+F32 = mybir.dt.float32
+BF16 = mybir.dt.bfloat16
+I32 = mybir.dt.int32
+U32 = mybir.dt.uint32
+U16 = mybir.dt.uint16
+U8 = mybir.dt.uint8
+FP8X4 = mybir.dt.float8_e4m3fn_x4
+MULT = mybir.AluOpType.mult
+ADD = mybir.AluOpType.add
+IDENT = mybir.ActivationFunctionType.Identity
+
+P = 128
+PASSES = 3
+GROUP = 4
+GROUPS = E // GROUP
+GSLOTS = GROUP * C
+TOK = 512
+
+
+def tile_moe_shr_lin_bias_kernel(tc, x_words, x_scales, w, b, gate, offs, pos1, pos2, out):
+    nc = tc.nc
+    with ExitStack() as ctx:
+        keep = ctx.enter_context(tc.tile_pool(name="keep", bufs=1))
+        psum = ctx.enter_context(tc.psum_pool(name="psum", bufs=1))
+
+        offs_sb = keep.tile([P, S // 16], U16, name="offs_sb")
+        pos_sb = [keep.tile([P, T // 16], U16, name="pos%d" % i) for i in range(2)]
+        xw = [keep.tile([P, T], I32, name="xw%d" % o, align_bytes=64) for o in range(PASSES)]
+        xs = keep.tile([P, T], U8, name="xs", align_bytes=64)
+        bias = keep.tile([P, E + 1], F32, name="bias")
+        gates = [keep.tile([P, T], F32, name="gate%d" % i) for i in range(2)]
+        y = keep.tile([P, S], F32, name="y")
+        gs = [keep.tile([P, GSLOTS], U8, name="gs%d" % g, align_bytes=64) for g in range(GROUPS)]
+        wq = [keep.tile([P, PASSES * N], U32, name="wq%d" % e, align_bytes=64) for e in range(E + 1)]
+        ws = [keep.tile([P, PASSES * N], U8, name="ws%d" % e, align_bytes=64) for e in range(E + 1)]
+        raw = [keep.tile([P, PASSES, 4, N], F32, name="raw%d" % e) for e in range(E + 1)]
+
+        def load_w(e):
+            nc.sync.dma_start(out=raw[e][:], in_=w[e].rearrange("(o p r) n -> p o r n", o=PASSES, r=4))
+
+        def load_x(o):
+            nc.sync.dma_start(out=xw[o][:], in_=x_words[o].rearrange("p t r -> p (t r)").bitcast(I32))
+
+        def load_scales():
+            for q in range(4):
+                nc.sync.dma_start(
+                    out=xs[32 * q : 32 * q + 4 * PASSES, :].bitcast(I32),
+                    in_=x_scales[:, 4 * q : 4 * q + 4, :].bitcast(I32),
+                )
+
+        nc.vector.memset(xs[:].bitcast(I32), 0)
+        nc.sync.dma_start(offs_sb[:], offs)
+        load_x(0)
+        load_scales()
+        for e in (E, 0, 1, 2):
+            load_w(e)
+        load_x(1)
+        load_w(3)
+        load_x(2)
+        for e in range(4, E):
+            load_w(e)
+        nc.sync.dma_start(bias[:], b)
+        nc.sync.dma_start(pos_sb[0][:], pos1)
+        nc.sync.dma_start(pos_sb[1][:], pos2)
+        for i in range(2):
+            nc.sync.dma_start(gates[i][:], gate[i])
+
+        stage = {}
+
+        def cast(e):
+            stage[e] = keep.tile([P, PASSES * N * 4], BF16, name="stage%d" % e, tag="hold%d" % e, align_bytes=64)
+            nc.scalar.copy(
+                out=stage[e][:].rearrange("p (o c i r) -> p o c r i", o=PASSES, i=4, r=4),
+                in_=raw[e][:].rearrange("p o r (c i) -> p o c r i", i=4),
+            )
+
+        def quantize(e):
+            for lo, hi in ((0, 2 * N), (2 * N, 3 * N)):
+                nc.vector.quantize_mx(
+                    out=wq[e][:, lo:hi].bitcast(FP8X4), scales=ws[e][:, lo:hi], in_=stage[e][:, 4 * lo : 4 * hi]
+                )
+
+        gw = {}
+
+        def gather_words(g, o, tag, cuts):
+            gw[g, o] = keep.tile([P, GSLOTS], U32, name="gw%d_%d" % (g, o), tag=tag, align_bytes=64)
+            for lo, hi in cuts:
+                nc.vector.tensor_copy(
+                    gw[g, o][:, lo:hi],
+                    xw[o][:].bitcast(U32).indirect(offs_sb[:, (g * GSLOTS + lo) // 16 : (g * GSLOTS + hi) // 16]),
+                )
+
+        def gather_scales(g):
+            nc.vector.tensor_copy(gs[g][:], xs[:].indirect(offs_sb[:, g * GSLOTS // 16 : (g + 1) * GSLOTS // 16]))
+
+        def product(e, acc, o):
+            g, j = divmod(e, GROUP)
+            nc.tensor.matmul_mx(
+                out=acc,
+                lhsT=wq[e][:, o * N : (o + 1) * N].bitcast(FP8X4),
+                lhsT_scale=ws[e][:, o * N : (o + 1) * N],
+                rhs=gw[g, o][:, j * C : (j + 1) * C].bitcast(FP8X4),
+                rhs_scale=gs[g][4 * o : P, j * C : (j + 1) * C],
+                start=(o == 0),
+                stop=(o == PASSES - 1),
+            )
+
+        def empty_scalar(e, acc):
+            nc.scalar.activation(out=y[:, e * C : (e + 1) * C], in_=acc, func=IDENT, bias=bias[:, e : e + 1])
+
+        whole = [(0, GSLOTS)]
+        for g in range(GROUPS):
+            gather_words(g, 0, "gw%d_0" % g, whole)
+        for g in range(GROUPS):
+            gather_scales(g)
+
+        cast(E)
+        quantize(E)
+        ys = []
+        for c in range(T // TOK):
+            acc = psum.tile([P, TOK], F32, name="ys%d" % c, tag="bank%d" % (4 + c))
+            ys.append(acc)
+            for o in range(PASSES):
+                nc.tensor.matmul_mx(
+                    out=acc[:],
+                    lhsT=wq[E][:, o * N : (o + 1) * N].bitcast(FP8X4),
+                    lhsT_scale=ws[E][:, o * N : (o + 1) * N],
+                    rhs=xw[o][:, c * TOK : (c + 1) * TOK].bitcast(FP8X4),
+                    rhs_scale=xs[4 * o : P, c * TOK : (c + 1) * TOK],
+                    start=(o == 0),
+                    stop=(o == PASSES - 1),
+                )
+
+        for g in range(GROUPS):
+            first = g * GROUP
+            for e in range(first, first + GROUP):
+                cast(e)
+                quantize(e)
+                if e == first + GROUP - 2:
+                    gather_words(g, 1, "hold%d" % e, whole)
+            last_group = g == GROUPS - 1
+            gather_words(g, 2, "hold%d" % (first + GROUP - 1), [(0, 2 * C), (2 * C, 3 * C), (3 * C, 4 * C)] if last_group else whole)
+            if not last_group:
+                for h in range(GROUP // 2):
+                    pair = psum.tile([P, 2, C], F32, name="pair%d_%d" % (g, h), tag="bank%d" % (2 * g + h))
+                    for j in range(2):
+                        for o in range(PASSES):
+                            product(first + 2 * h + j, pair[:, j, :], o)
+                    for j in range(2):
+                        empty_scalar(first + 2 * h + j, pair[:, j, :])
+            else:
+                accs = [psum.tile([P, C], F32, name="acc%d" % j, tag="bank%d" % ((7 + j) % 8)) for j in range(GROUP)]
+                for o in range(PASSES - 1):
+                    for j in range(GROUP):
+                        product(first + j, accs[j][:], o)
+                for j in range(GROUP):
+                    e = first + j
+                    product(e, accs[j][:], PASSES - 1)
+                    if j < GROUP - 1:
+                        empty_scalar(e, accs[j][:])
+                    else:
+                        nc.vector.tensor_scalar_add(y[:, e * C : (e + 1) * C], accs[j][:], bias[:, e : e + 1])
+
+        ident = keep.tile([P, P], F32, name="ident")
+        make_identity(nc, ident[:])
+        edges = (0, 512, 896, 1152, 1536)
+        chunks = list(zip(edges[:-1], edges[1:]))
+        turned_end = edges[-2]
+        ys_sb = keep.tile([P, turned_end], F32, name="ys_sb")
+        for c in range(T // TOK):
+            hi = min(turned_end, (c + 1) * TOK)
+            if hi > c * TOK:
+                nc.scalar.activation(
+                    out=ys_sb[:, c * TOK : hi], in_=ys[c][:, 0 : hi - c * TOK], func=IDENT, bias=bias[:, E : E + 1]
+                )
+
+        def pick(i, lo, hi):
+            picked = keep.tile([P, hi - lo], F32, name="pick%d_%d" % (i, lo))
+            nc.vector.tensor_tensor(
+                picked[:], y[:].indirect(pos_sb[i][:, lo // 16 : hi // 16]), gates[i][:, lo:hi], MULT
+            )
+            return picked
+
+        sum_banks = (3, 0, 1)
+        back_banks = (7, 2, 4)
+        for c, (lo, hi) in enumerate(chunks[:-1]):
+            width = hi - lo
+            terms = [ys_sb[:, lo:hi], pick(0, lo, hi)[:], pick(1, lo, hi)[:]]
+            blocks = width // P
+            total = psum.tile([P, width], F32, name="total%d" % c, tag="bank%d" % sum_banks[c])
+            for i, term in enumerate(terms):
+                for k in range(blocks):
+                    nc.tensor.matmul(
+                        total[:, k * P : (k + 1) * P], term[:, k * P : (k + 1) * P], ident[:], is_transpose=True,
+                        start=(i == 0 and k == 0), stop=(i == 2 and k == blocks - 1),
+                    )
+            turned = keep.tile([P, width], F32, name="turned%d" % c)
+            nc.scalar.copy(out=turned[:], in_=total[:])
+            back = psum.tile([P, width], F32, name="back%d" % c, tag="bank%d" % back_banks[c])
+            for k in range(blocks):
+                nc.tensor.transpose(back[:, k * P : (k + 1) * P], turned[:, k * P : (k + 1) * P], ident[:])
+            res = keep.tile([P, width], F32, name="res%d" % c)
+            nc.scalar.copy(out=res[:], in_=back[:])
+            nc.sync.dma_start(out=out[:, lo:hi], in_=res[:])
+
+        lo, hi = chunks[-1]
+        first_pick = pick(0, lo, hi)
+        second_pick = pick(1, lo, hi)
+        part = keep.tile([P, hi - lo], F32, name="part")
+        nc.vector.scalar_tensor_tensor(
+            out=part[:], in0=ys[lo // TOK][:, lo % TOK : TOK], scalar=bias[:, E : E + 1], in1=first_pick[:], op0=ADD, op1=ADD
+        )
+        res = keep.tile([P, hi - lo], F32, name="res_last")
+        nc.vector.tensor_tensor(res[:], part[:], second_pick[:], ADD)
+        nc.sync.dma_start(out=out[:, lo:hi], in_=res[:])

@@ -23,7 +23,7 @@ PASSES = 3
 GROUP = 4
 GROUPS = E // GROUP
 GSLOTS = GROUP * C
-TOK = 512
+BANK = 512
 
 
 def tile_moe_shr_lin_bias_kernel(tc, x_words, x_scales, w, b, gate, offs, pos1, pos2, out):
@@ -32,20 +32,28 @@ def tile_moe_shr_lin_bias_kernel(tc, x_words, x_scales, w, b, gate, offs, pos1, 
         keep = ctx.enter_context(tc.tile_pool(name="keep", bufs=1))
         psum = ctx.enter_context(tc.psum_pool(name="psum", bufs=1))
 
+        edges = (0, 512, 896, 1152, 1536)
+        chunks = list(zip(edges[:-1], edges[1:]))
+        turned_end = edges[-2]
+
         offs_sb = keep.tile([P, S // 16], U16, name="offs_sb")
         pos_sb = [keep.tile([P, T // 16], U16, name="pos%d" % i) for i in range(2)]
         xw = [keep.tile([P, T], I32, name="xw%d" % o, align_bytes=64) for o in range(PASSES)]
         xs = keep.tile([P, T], U8, name="xs", align_bytes=64)
         bias = keep.tile([P, E + 1], F32, name="bias")
         gates = [keep.tile([P, T], F32, name="gate%d" % i) for i in range(2)]
-        y = keep.tile([P, S], F32, name="y")
-        gs = [keep.tile([P, GSLOTS], U8, name="gs%d" % g, align_bytes=64) for g in range(GROUPS)]
+        ident = keep.tile([P, P], F32, name="ident")
         wq = [keep.tile([P, PASSES * N], U32, name="wq%d" % e, align_bytes=64) for e in range(E + 1)]
         ws = [keep.tile([P, PASSES * N], U8, name="ws%d" % e, align_bytes=64) for e in range(E + 1)]
-        raw = [keep.tile([P, PASSES, 4, N], F32, name="raw%d" % e) for e in range(E + 1)]
+        raw = [keep.tile([P, PASSES, 4, N], F32, name="raw%d" % e, tag="raw%d" % e) for e in range(E + 1)]
+
+        def pass_cuts(e):
+            return [(o, o + 1) for o in range(PASSES)] if e == E - 1 else [(0, PASSES)]
 
         def load_w(e):
-            nc.sync.dma_start(out=raw[e][:], in_=w[e].rearrange("(o p r) n -> p o r n", o=PASSES, r=4))
+            rows = w[e].rearrange("(o p r) n -> p o r n", o=PASSES, r=4)
+            for lo, hi in pass_cuts(e):
+                nc.sync.dma_start(out=raw[e][:, lo:hi], in_=rows[:, lo:hi])
 
         def load_x(o):
             nc.sync.dma_start(out=xw[o][:], in_=x_words[o].rearrange("p t r -> p (t r)").bitcast(I32))
@@ -57,18 +65,20 @@ def tile_moe_shr_lin_bias_kernel(tc, x_words, x_scales, w, b, gate, offs, pos1, 
                     in_=x_scales[:, 4 * q : 4 * q + 4, :].bitcast(I32),
                 )
 
-        nc.vector.memset(xs[:].bitcast(I32), 0)
+        nc.gpsimd.memset(xs[:].bitcast(I32), 0)
+        make_identity(nc, ident[:])
         nc.sync.dma_start(offs_sb[:], offs)
         load_x(0)
-        load_scales()
-        for e in (E, 0, 1, 2):
-            load_w(e)
+        load_w(E)
+        load_w(0)
         load_x(1)
-        load_w(3)
+        for e in (1, 2, 3):
+            load_w(e)
+        load_scales()
         load_x(2)
+        nc.sync.dma_start(bias[:], b)
         for e in range(4, E):
             load_w(e)
-        nc.sync.dma_start(bias[:], b)
         nc.sync.dma_start(pos_sb[0][:], pos1)
         nc.sync.dma_start(pos_sb[1][:], pos2)
         for i in range(2):
@@ -78,10 +88,11 @@ def tile_moe_shr_lin_bias_kernel(tc, x_words, x_scales, w, b, gate, offs, pos1, 
 
         def cast(e):
             stage[e] = keep.tile([P, PASSES * N * 4], BF16, name="stage%d" % e, tag="hold%d" % e, align_bytes=64)
-            nc.scalar.copy(
-                out=stage[e][:].rearrange("p (o c i r) -> p o c r i", o=PASSES, i=4, r=4),
-                in_=raw[e][:].rearrange("p o r (c i) -> p o c r i", i=4),
-            )
+            for lo, hi in pass_cuts(e):
+                nc.scalar.copy(
+                    out=stage[e][:, lo * 4 * N : hi * 4 * N].rearrange("p (o c i r) -> p o c r i", o=hi - lo, i=4, r=4),
+                    in_=raw[e][:, lo:hi].rearrange("p o r (c i) -> p o c r i", i=4),
+                )
 
         def quantize(e):
             for lo, hi in ((0, 2 * N), (2 * N, 3 * N)):
@@ -90,6 +101,7 @@ def tile_moe_shr_lin_bias_kernel(tc, x_words, x_scales, w, b, gate, offs, pos1, 
                 )
 
         gw = {}
+        gs = {}
 
         def gather_words(g, o, tag, cuts):
             gw[g, o] = keep.tile([P, GSLOTS], U32, name="gw%d_%d" % (g, o), tag=tag, align_bytes=64)
@@ -99,88 +111,107 @@ def tile_moe_shr_lin_bias_kernel(tc, x_words, x_scales, w, b, gate, offs, pos1, 
                     xw[o][:].bitcast(U32).indirect(offs_sb[:, (g * GSLOTS + lo) // 16 : (g * GSLOTS + hi) // 16]),
                 )
 
-        def gather_scales(g):
+        def gather_scales(g, tag):
+            gs[g] = keep.tile([P, GSLOTS], U8, name="gs%d" % g, tag=tag, align_bytes=64)
             nc.vector.tensor_copy(gs[g][:], xs[:].indirect(offs_sb[:, g * GSLOTS // 16 : (g + 1) * GSLOTS // 16]))
 
         def product(e, acc, o):
             g, j = divmod(e, GROUP)
+            words = gw[g, o][:, j * C : (j + 1) * C] if (g, o) in gw else last_words[e]
             nc.tensor.matmul_mx(
                 out=acc,
                 lhsT=wq[e][:, o * N : (o + 1) * N].bitcast(FP8X4),
                 lhsT_scale=ws[e][:, o * N : (o + 1) * N],
-                rhs=gw[g, o][:, j * C : (j + 1) * C].bitcast(FP8X4),
+                rhs=words.bitcast(FP8X4),
                 rhs_scale=gs[g][4 * o : P, j * C : (j + 1) * C],
                 start=(o == 0),
                 stop=(o == PASSES - 1),
             )
 
-        def empty_scalar(e, acc):
-            nc.scalar.activation(out=y[:, e * C : (e + 1) * C], in_=acc, func=IDENT, bias=bias[:, e : e + 1])
-
         whole = [(0, GSLOTS)]
-        for g in range(GROUPS):
-            gather_words(g, 0, "gw%d_0" % g, whole)
-        for g in range(GROUPS):
-            gather_scales(g)
+        for o in range(2):
+            for g in range(GROUPS):
+                gather_words(g, o, "gw%d_%d" % (g, o), whole)
 
         cast(E)
         quantize(E)
-        ys = []
-        for c in range(T // TOK):
-            acc = psum.tile([P, TOK], F32, name="ys%d" % c, tag="bank%d" % (4 + c))
-            ys.append(acc)
+        shared_banks = []
+        for c in range(T // BANK):
+            acc = psum.tile([P, BANK], F32, name="shared%d" % c, tag="bank%d" % (4 + c))
+            shared_banks.append(acc)
             for o in range(PASSES):
                 nc.tensor.matmul_mx(
                     out=acc[:],
                     lhsT=wq[E][:, o * N : (o + 1) * N].bitcast(FP8X4),
                     lhsT_scale=ws[E][:, o * N : (o + 1) * N],
-                    rhs=xw[o][:, c * TOK : (c + 1) * TOK].bitcast(FP8X4),
-                    rhs_scale=xs[4 * o : P, c * TOK : (c + 1) * TOK],
+                    rhs=xw[o][:, c * BANK : (c + 1) * BANK].bitcast(FP8X4),
+                    rhs_scale=xs[4 * o : P, c * BANK : (c + 1) * BANK],
                     start=(o == 0),
                     stop=(o == PASSES - 1),
                 )
 
-        for g in range(GROUPS):
+        pairs = []
+        for g in range(GROUPS - 1):
             first = g * GROUP
             for e in range(first, first + GROUP):
                 cast(e)
                 quantize(e)
                 if e == first + GROUP - 2:
-                    gather_words(g, 1, "hold%d" % e, whole)
-            last_group = g == GROUPS - 1
-            gather_words(g, 2, "hold%d" % (first + GROUP - 1), [(0, 2 * C), (2 * C, 3 * C), (3 * C, 4 * C)] if last_group else whole)
-            if not last_group:
-                for h in range(GROUP // 2):
-                    pair = psum.tile([P, 2, C], F32, name="pair%d_%d" % (g, h), tag="bank%d" % (2 * g + h))
-                    for j in range(2):
-                        for o in range(PASSES):
-                            product(first + 2 * h + j, pair[:, j, :], o)
-                    for j in range(2):
-                        empty_scalar(first + 2 * h + j, pair[:, j, :])
-            else:
-                accs = [psum.tile([P, C], F32, name="acc%d" % j, tag="bank%d" % ((7 + j) % 8)) for j in range(GROUP)]
-                for o in range(PASSES - 1):
-                    for j in range(GROUP):
-                        product(first + j, accs[j][:], o)
-                for j in range(GROUP):
-                    e = first + j
-                    product(e, accs[j][:], PASSES - 1)
-                    if j < GROUP - 1:
-                        empty_scalar(e, accs[j][:])
-                    else:
-                        nc.vector.tensor_scalar_add(y[:, e * C : (e + 1) * C], accs[j][:], bias[:, e : e + 1])
+                    gather_scales(g, "hold%d" % e)
+            gather_words(g, 2, "hold%d" % (first + GROUP - 1), whole)
+            for h in range(GROUP // 2):
+                pair = psum.tile([P, 2, C], F32, name="pair%d_%d" % (g, h), tag="bank%d" % (2 * g + h))
+                pairs.append(pair)
+                for j in range(2):
+                    for o in range(PASSES):
+                        product(first + 2 * h + j, pair[:, j, :], o)
 
-        ident = keep.tile([P, P], F32, name="ident")
-        make_identity(nc, ident[:])
-        edges = (0, 512, 896, 1152, 1536)
-        chunks = list(zip(edges[:-1], edges[1:]))
-        turned_end = edges[-2]
-        ys_sb = keep.tile([P, turned_end], F32, name="ys_sb")
-        for c in range(T // TOK):
-            hi = min(turned_end, (c + 1) * TOK)
-            if hi > c * TOK:
+        last_words = {}
+
+        def gather_last(experts, tag):
+            words = keep.tile([P, len(experts), C], U32, name="last%d" % experts[0], tag=tag, align_bytes=64)
+            for j, e in enumerate(experts):
+                last_words[e] = words[:, j, :]
+                nc.vector.tensor_copy(
+                    words[:, j, :], xw[PASSES - 1][:].bitcast(U32).indirect(offs_sb[:, e * C // 16 : (e + 1) * C // 16])
+                )
+
+        first = E - GROUP
+        for e in range(first, E):
+            cast(e)
+            quantize(e)
+            if e == first:
+                gather_scales(GROUPS - 1, "hold%d" % e)
+            else:
+                gather_last([e - 1] if e < E - 1 else [e - 1, e], "hold%d" % e)
+
+        y = keep.tile([P, S], F32, name="y", tag="raw%d" % (E - 1))
+
+        def empty_scalar(e, acc):
+            nc.scalar.activation(out=y[:, e * C : (e + 1) * C], in_=acc, func=IDENT, bias=bias[:, e : e + 1])
+
+        for e in range(E - GROUP):
+            empty_scalar(e, pairs[e // 2][:, e % 2, :])
+
+        first = E - GROUP
+        accs = [psum.tile([P, C], F32, name="acc%d" % j, tag="bank%d" % ((7 + j) % 8)) for j in range(GROUP)]
+        for o in range(PASSES - 1):
+            for j in range(GROUP):
+                product(first + j, accs[j][:], o)
+        for j in range(GROUP):
+            e = first + j
+            product(e, accs[j][:], PASSES - 1)
+            if j < GROUP - 1:
+                empty_scalar(e, accs[j][:])
+            else:
+                nc.vector.tensor_scalar_add(y[:, e * C : (e + 1) * C], accs[j][:], bias[:, e : e + 1])
+
+        shared = keep.tile([P, turned_end], F32, name="shared", tag="hold%d" % (E - 1), align_bytes=64)
+        for c in range(T // BANK):
+            lo, hi = c * BANK, min(turned_end, (c + 1) * BANK)
+            if hi > lo:
                 nc.scalar.activation(
-                    out=ys_sb[:, c * TOK : hi], in_=ys[c][:, 0 : hi - c * TOK], func=IDENT, bias=bias[:, E : E + 1]
+                    out=shared[:, lo:hi], in_=shared_banks[c][:, 0 : hi - lo], func=IDENT, bias=bias[:, E : E + 1]
                 )
 
         def pick(i, lo, hi):
@@ -190,11 +221,11 @@ def tile_moe_shr_lin_bias_kernel(tc, x_words, x_scales, w, b, gate, offs, pos1, 
             )
             return picked
 
-        sum_banks = (3, 0, 1)
-        back_banks = (7, 2, 4)
+        sum_banks = (3, 0, 2)
+        back_banks = (7, 1, 4)
         for c, (lo, hi) in enumerate(chunks[:-1]):
             width = hi - lo
-            terms = [ys_sb[:, lo:hi], pick(0, lo, hi)[:], pick(1, lo, hi)[:]]
+            terms = [shared[:, lo:hi], pick(0, lo, hi)[:], pick(1, lo, hi)[:]]
             blocks = width // P
             total = psum.tile([P, width], F32, name="total%d" % c, tag="bank%d" % sum_banks[c])
             for i, term in enumerate(terms):
@@ -217,7 +248,7 @@ def tile_moe_shr_lin_bias_kernel(tc, x_words, x_scales, w, b, gate, offs, pos1, 
         second_pick = pick(1, lo, hi)
         part = keep.tile([P, hi - lo], F32, name="part")
         nc.vector.scalar_tensor_tensor(
-            out=part[:], in0=ys[lo // TOK][:, lo % TOK : TOK], scalar=bias[:, E : E + 1], in1=first_pick[:], op0=ADD, op1=ADD
+            out=part[:], in0=shared_banks[lo // BANK][:, lo % BANK : BANK], scalar=bias[:, E : E + 1], in1=first_pick[:], op0=ADD, op1=ADD
         )
         res = keep.tile([P, hi - lo], F32, name="res_last")
         nc.vector.tensor_tensor(res[:], part[:], second_pick[:], ADD)

@@ -90,8 +90,8 @@ def tile_moe_shr_lin_bias_kernel(tc, x_words, x_scales, w, b, gate, offs, pos1, 
             stage[e] = keep.tile([P, PASSES * N * 4], BF16, name="stage%d" % e, tag="hold%d" % e, align_bytes=64)
             for lo, hi in pass_cuts(e):
                 nc.scalar.copy(
-                    out=stage[e][:, lo * 4 * N : hi * 4 * N].rearrange("p (o c i r) -> p o c r i", o=hi - lo, i=4, r=4),
-                    in_=raw[e][:, lo:hi].rearrange("p o r (c i) -> p o c r i", i=4),
+                    out=stage[e][:, lo * 4 * N : hi * 4 * N].rearrange("p (o c i r) -> p o c r i", o=hi - lo, i=2, r=4),
+                    in_=raw[e][:, lo:hi].rearrange("p o r (c i) -> p o c r i", i=2),
                 )
 
         def quantize(e):

@@ -45,15 +45,18 @@ def tile_moe_shr_lin_bias_kernel(tc, x_words, x_scales, w, b, gate, offs, pos1, 
         ident = keep.tile([P, P], F32, name="ident")
         wq = [keep.tile([P, PASSES * N], U32, name="wq%d" % e, align_bytes=64) for e in range(E + 1)]
         ws = [keep.tile([P, PASSES * N], U8, name="ws%d" % e, align_bytes=64) for e in range(E + 1)]
-        raw = [keep.tile([P, PASSES, 4, N], F32, name="raw%d" % e, tag="raw%d" % e) for e in range(E + 1)]
-
         def pass_cuts(e):
             return [(o, o + 1) for o in range(PASSES)] if e == E - 1 else [(0, PASSES)]
+
+        raw = {}
+        for e in range(E + 1):
+            for lo, hi in pass_cuts(e):
+                raw[e, hi] = keep.tile([P, hi - lo, 4, N], F32, name="raw%d_%d" % (e, hi), tag="raw%d_%d" % (e, hi), align_bytes=64)
 
         def load_w(e):
             rows = w[e].rearrange("(o p r) n -> p o r n", o=PASSES, r=4)
             for lo, hi in pass_cuts(e):
-                nc.sync.dma_start(out=raw[e][:, lo:hi], in_=rows[:, lo:hi])
+                nc.sync.dma_start(out=raw[e, hi][:], in_=rows[:, lo:hi])
 
         def load_x(o):
             nc.sync.dma_start(out=xw[o][:], in_=x_words[o].rearrange("p t r -> p (t r)").bitcast(I32))
@@ -69,15 +72,15 @@ def tile_moe_shr_lin_bias_kernel(tc, x_words, x_scales, w, b, gate, offs, pos1, 
         make_identity(nc, ident[:])
         nc.sync.dma_start(offs_sb[:], offs)
         load_x(0)
-        load_w(E)
         load_w(0)
+        load_w(1)
         load_x(1)
-        for e in (1, 2, 3):
+        for e in (2, 3, 4):
             load_w(e)
         load_scales()
         load_x(2)
         nc.sync.dma_start(bias[:], b)
-        for e in range(4, E):
+        for e in range(5, E + 1):
             load_w(e)
         nc.sync.dma_start(pos_sb[0][:], pos1)
         nc.sync.dma_start(pos_sb[1][:], pos2)
@@ -87,11 +90,11 @@ def tile_moe_shr_lin_bias_kernel(tc, x_words, x_scales, w, b, gate, offs, pos1, 
         stage = {}
 
         def cast(e):
-            stage[e] = keep.tile([P, PASSES * N * 4], BF16, name="stage%d" % e, tag="hold%d" % e, align_bytes=64)
+            stage[e] = keep.tile([P, PASSES * N * 4], BF16, name="stage%d" % e, align_bytes=64)
             for lo, hi in pass_cuts(e):
                 nc.scalar.copy(
                     out=stage[e][:, lo * 4 * N : hi * 4 * N].rearrange("p (o c i r) -> p o c r i", o=hi - lo, i=2, r=4),
-                    in_=raw[e][:, lo:hi].rearrange("p o r (c i) -> p o c r i", i=2),
+                    in_=raw[e, hi][:].rearrange("p o r (c i) -> p o c r i", i=2),
                 )
 
         def quantize(e):
@@ -133,23 +136,6 @@ def tile_moe_shr_lin_bias_kernel(tc, x_words, x_scales, w, b, gate, offs, pos1, 
             for g in range(GROUPS):
                 gather_words(g, o, "gw%d_%d" % (g, o), whole)
 
-        cast(E)
-        quantize(E)
-        shared_banks = []
-        for c in range(T // BANK):
-            acc = psum.tile([P, BANK], F32, name="shared%d" % c, tag="bank%d" % (4 + c))
-            shared_banks.append(acc)
-            for o in range(PASSES):
-                nc.tensor.matmul_mx(
-                    out=acc[:],
-                    lhsT=wq[E][:, o * N : (o + 1) * N].bitcast(FP8X4),
-                    lhsT_scale=ws[E][:, o * N : (o + 1) * N],
-                    rhs=xw[o][:, c * BANK : (c + 1) * BANK].bitcast(FP8X4),
-                    rhs_scale=xs[4 * o : P, c * BANK : (c + 1) * BANK],
-                    start=(o == 0),
-                    stop=(o == PASSES - 1),
-                )
-
         pairs = []
         for g in range(GROUPS - 1):
             first = g * GROUP
@@ -157,8 +143,8 @@ def tile_moe_shr_lin_bias_kernel(tc, x_words, x_scales, w, b, gate, offs, pos1, 
                 cast(e)
                 quantize(e)
                 if e == first + GROUP - 2:
-                    gather_scales(g, "hold%d" % e)
-            gather_words(g, 2, "hold%d" % (first + GROUP - 1), whole)
+                    gather_scales(g, "raw%d_%d" % (e, PASSES))
+            gather_words(g, 2, "raw%d_%d" % (first + GROUP - 1, PASSES), whole)
             for h in range(GROUP // 2):
                 pair = psum.tile([P, 2, C], F32, name="pair%d_%d" % (g, h), tag="bank%d" % (2 * g + h))
                 pairs.append(pair)
@@ -181,11 +167,11 @@ def tile_moe_shr_lin_bias_kernel(tc, x_words, x_scales, w, b, gate, offs, pos1, 
             cast(e)
             quantize(e)
             if e == first:
-                gather_scales(GROUPS - 1, "hold%d" % e)
+                gather_scales(GROUPS - 1, "raw%d_%d" % (e, PASSES))
             else:
-                gather_last([e - 1] if e < E - 1 else [e - 1, e], "hold%d" % e)
+                gather_last([e - 1] if e < E - 1 else [e - 1, e], "raw%d_%d" % (e, PASSES))
 
-        y = keep.tile([P, S], F32, name="y", tag="raw%d" % (E - 1))
+        y = keep.tile([P, S], F32, name="y", tag="raw%d_%d" % (E - 1, PASSES - 1), align_bytes=64)
 
         def empty_scalar(e, acc):
             nc.scalar.activation(out=y[:, e * C : (e + 1) * C], in_=acc, func=IDENT, bias=bias[:, e : e + 1])
@@ -193,20 +179,35 @@ def tile_moe_shr_lin_bias_kernel(tc, x_words, x_scales, w, b, gate, offs, pos1, 
         for e in range(E - GROUP):
             empty_scalar(e, pairs[e // 2][:, e % 2, :])
 
+        cast(E)
+
         first = E - GROUP
-        accs = [psum.tile([P, C], F32, name="acc%d" % j, tag="bank%d" % ((7 + j) % 8)) for j in range(GROUP)]
+        accs = [psum.tile([P, C], F32, name="acc%d" % j, tag="bank%d" % (4 + j)) for j in range(GROUP)]
         for o in range(PASSES - 1):
             for j in range(GROUP):
                 product(first + j, accs[j][:], o)
         for j in range(GROUP):
             e = first + j
             product(e, accs[j][:], PASSES - 1)
-            if j < GROUP - 1:
-                empty_scalar(e, accs[j][:])
-            else:
-                nc.vector.tensor_scalar_add(y[:, e * C : (e + 1) * C], accs[j][:], bias[:, e : e + 1])
+            empty_scalar(e, accs[j][:])
 
-        shared = keep.tile([P, turned_end], F32, name="shared", tag="hold%d" % (E - 1), align_bytes=64)
+        quantize(E)
+        shared_banks = []
+        for c in range(T // BANK):
+            acc = psum.tile([P, BANK], F32, name="shared%d" % c, tag="bank%d" % c)
+            shared_banks.append(acc)
+            for o in range(PASSES):
+                nc.tensor.matmul_mx(
+                    out=acc[:],
+                    lhsT=wq[E][:, o * N : (o + 1) * N].bitcast(FP8X4),
+                    lhsT_scale=ws[E][:, o * N : (o + 1) * N],
+                    rhs=xw[o][:, c * BANK : (c + 1) * BANK].bitcast(FP8X4),
+                    rhs_scale=xs[4 * o : P, c * BANK : (c + 1) * BANK],
+                    start=(o == 0),
+                    stop=(o == PASSES - 1),
+                )
+
+        shared = keep.tile([P, turned_end], F32, name="shared", tag="raw0_%d" % PASSES, align_bytes=64)
         for c in range(T // BANK):
             lo, hi = c * BANK, min(turned_end, (c + 1) * BANK)
             if hi > lo:
@@ -221,8 +222,8 @@ def tile_moe_shr_lin_bias_kernel(tc, x_words, x_scales, w, b, gate, offs, pos1, 
             )
             return picked
 
-        sum_banks = (3, 0, 2)
-        back_banks = (7, 1, 4)
+        sum_banks = (3, 4, 5)
+        back_banks = (6, 7, 0)
         for c, (lo, hi) in enumerate(chunks[:-1]):
             width = hi - lo
             terms = [shared[:, lo:hi], pick(0, lo, hi)[:], pick(1, lo, hi)[:]]

@@ -35,6 +35,7 @@ def tile_moe_shr_lin_bias_kernel(tc, x_words, x_scales, w, b, gate, offs, pos1, 
         edges = (0, 512, 896, 1152, 1536)
         chunks = list(zip(edges[:-1], edges[1:]))
         turned_end = edges[-2]
+        sets = ((0, 2), (2, 6), (6, 10), (10, 11), (11, 12), (12, 13))
 
         offs_sb = keep.tile([P, S // 16], U16, name="offs_sb")
         pos_sb = [keep.tile([P, T // 16], U16, name="pos%d" % i) for i in range(2)]
@@ -43,20 +44,10 @@ def tile_moe_shr_lin_bias_kernel(tc, x_words, x_scales, w, b, gate, offs, pos1, 
         bias = keep.tile([P, E + 1], F32, name="bias")
         gates = [keep.tile([P, T], F32, name="gate%d" % i) for i in range(2)]
         ident = keep.tile([P, P], F32, name="ident")
-        wq = [keep.tile([P, PASSES * N], U32, name="wq%d" % e, align_bytes=64) for e in range(E + 1)]
-        ws = [keep.tile([P, PASSES * N], U8, name="ws%d" % e, align_bytes=64) for e in range(E + 1)]
-        def pass_cuts(e):
-            return [(o, o + 1) for o in range(PASSES)] if e == E - 1 else [(0, PASSES)]
-
-        raw = {}
-        for e in range(E + 1):
-            for lo, hi in pass_cuts(e):
-                raw[e, hi] = keep.tile([P, hi - lo, 4, N], F32, name="raw%d_%d" % (e, hi), tag="raw%d_%d" % (e, hi), align_bytes=64)
+        raw = [keep.tile([P, PASSES, 4, N], F32, name="raw%d" % e, align_bytes=64) for e in range(E + 1)]
 
         def load_w(e):
-            rows = w[e].rearrange("(o p r) n -> p o r n", o=PASSES, r=4)
-            for lo, hi in pass_cuts(e):
-                nc.sync.dma_start(out=raw[e, hi][:], in_=rows[:, lo:hi])
+            nc.sync.dma_start(out=raw[e][:], in_=w[e].rearrange("(o p r) n -> p o r n", o=PASSES, r=4))
 
         def load_x(o):
             nc.sync.dma_start(out=xw[o][:], in_=x_words[o].rearrange("p t r -> p (t r)").bitcast(I32))
@@ -68,40 +59,51 @@ def tile_moe_shr_lin_bias_kernel(tc, x_words, x_scales, w, b, gate, offs, pos1, 
                     in_=x_scales[:, 4 * q : 4 * q + 4, :].bitcast(I32),
                 )
 
-        nc.gpsimd.memset(xs[:].bitcast(I32), 0)
+        nc.vector.memset(xs[:].bitcast(I32), 0)
         make_identity(nc, ident[:])
-        nc.sync.dma_start(offs_sb[:], offs)
         load_x(0)
+        nc.sync.dma_start(offs_sb[:], offs)
         load_w(0)
-        load_w(1)
-        load_x(1)
-        for e in (2, 3, 4):
-            load_w(e)
-        load_scales()
-        load_x(2)
         nc.sync.dma_start(bias[:], b)
-        for e in range(5, E + 1):
+        load_scales()
+        for e in range(1, 6):
+            load_w(e)
+        load_x(1)
+        for e in range(6, 11):
+            load_w(e)
+        load_x(2)
+        for e in range(11, E + 1):
             load_w(e)
         nc.sync.dma_start(pos_sb[0][:], pos1)
         nc.sync.dma_start(pos_sb[1][:], pos2)
         for i in range(2):
             nc.sync.dma_start(gates[i][:], gate[i])
 
-        stage = {}
+        wq = {}
+        ws = {}
 
-        def cast(e):
-            stage[e] = keep.tile([P, PASSES * N * 4], BF16, name="stage%d" % e, align_bytes=64)
-            for lo, hi in pass_cuts(e):
+        def quantize(first, end):
+            words = (end - first) * PASSES * N
+            stage = keep.tile([P, 4 * words], BF16, name="stage%d" % first, align_bytes=64)
+            codes = keep.tile([P, words], U32, name="wq%d" % first, align_bytes=64)
+            scales = keep.tile([P, words], U8, name="ws%d" % first, align_bytes=64)
+            for e in range(first, end):
+                lo, hi = (e - first) * PASSES * N, (e - first + 1) * PASSES * N
+                wq[e] = codes[:, lo:hi]
+                ws[e] = scales[:, lo:hi]
                 nc.scalar.copy(
-                    out=stage[e][:, lo * 4 * N : hi * 4 * N].rearrange("p (o c i r) -> p o c r i", o=hi - lo, i=2, r=4),
-                    in_=raw[e, hi][:].rearrange("p o r (c i) -> p o c r i", i=2),
+                    out=stage[:, 4 * lo : 4 * hi].rearrange("p (o c i r) -> p o c r i", o=PASSES, i=2, r=4),
+                    in_=raw[e][:].rearrange("p o r (c i) -> p o c r i", i=2),
                 )
-
-        def quantize(e):
-            for lo, hi in ((0, 2 * N), (2 * N, 3 * N)):
-                nc.vector.quantize_mx(
-                    out=wq[e][:, lo:hi].bitcast(FP8X4), scales=ws[e][:, lo:hi], in_=stage[e][:, 4 * lo : 4 * hi]
-                )
+            lo = 0
+            for width in (1024, 512, 256, 128):
+                while words - lo >= width:
+                    nc.vector.quantize_mx(
+                        out=codes[:, lo : lo + width].bitcast(FP8X4),
+                        scales=scales[:, lo : lo + width],
+                        in_=stage[:, 4 * lo : 4 * (lo + width)],
+                    )
+                    lo = lo + width
 
         gw = {}
         gs = {}
@@ -114,84 +116,54 @@ def tile_moe_shr_lin_bias_kernel(tc, x_words, x_scales, w, b, gate, offs, pos1, 
                     xw[o][:].bitcast(U32).indirect(offs_sb[:, (g * GSLOTS + lo) // 16 : (g * GSLOTS + hi) // 16]),
                 )
 
-        def gather_scales(g, tag):
-            gs[g] = keep.tile([P, GSLOTS], U8, name="gs%d" % g, tag=tag, align_bytes=64)
+        def gather_scales(g):
+            gs[g] = keep.tile([P, GSLOTS], U8, name="gs%d" % g, align_bytes=64)
             nc.vector.tensor_copy(gs[g][:], xs[:].indirect(offs_sb[:, g * GSLOTS // 16 : (g + 1) * GSLOTS // 16]))
 
         def product(e, acc, o):
             g, j = divmod(e, GROUP)
-            words = gw[g, o][:, j * C : (j + 1) * C] if (g, o) in gw else last_words[e]
             nc.tensor.matmul_mx(
                 out=acc,
                 lhsT=wq[e][:, o * N : (o + 1) * N].bitcast(FP8X4),
                 lhsT_scale=ws[e][:, o * N : (o + 1) * N],
-                rhs=words.bitcast(FP8X4),
+                rhs=gw[g, o][:, j * C : (j + 1) * C].bitcast(FP8X4),
                 rhs_scale=gs[g][4 * o : P, j * C : (j + 1) * C],
                 start=(o == 0),
                 stop=(o == PASSES - 1),
             )
 
         whole = [(0, GSLOTS)]
-        for o in range(2):
-            for g in range(GROUPS):
-                gather_words(g, o, "gw%d_%d" % (g, o), whole)
-
-        pairs = []
+        for g in range(GROUPS):
+            gather_words(g, 0, "gw%d_0" % g, whole)
+        for g in range(GROUPS):
+            gather_scales(g)
+        quantize(*sets[0])
+        quantize(*sets[1])
+        for g in range(GROUPS):
+            gather_words(g, 1, "gw%d_1" % g, whole)
+        quantize(*sets[2])
+        quantize(*sets[3])
         for g in range(GROUPS - 1):
-            first = g * GROUP
-            for e in range(first, first + GROUP):
-                cast(e)
-                quantize(e)
-                if e == first + GROUP - 2:
-                    gather_scales(g, "raw%d_%d" % (e, PASSES))
-            gather_words(g, 2, "raw%d_%d" % (first + GROUP - 1, PASSES), whole)
-            for h in range(GROUP // 2):
-                pair = psum.tile([P, 2, C], F32, name="pair%d_%d" % (g, h), tag="bank%d" % (2 * g + h))
-                pairs.append(pair)
-                for j in range(2):
-                    for o in range(PASSES):
-                        product(first + 2 * h + j, pair[:, j, :], o)
+            gather_words(g, 2, "gw%d_2" % g, whole)
+        quantize(*sets[4])
+        gather_words(GROUPS - 1, 2, "raw%d" % (E - 1), [(0, 2 * C), (2 * C, 3 * C), (3 * C, 4 * C)])
+        quantize(*sets[5])
 
-        last_words = {}
+        accs = []
+        for h in range(E // 2 - 1):
+            pair = psum.tile([P, 2, C], F32, name="pair%d" % h, tag="bank%d" % h)
+            accs.extend([pair[:, 0, :], pair[:, 1, :]])
+        for j in range(2):
+            lone = psum.tile([P, C], F32, name="lone%d" % j, tag="bank%d" % (E // 2 - 1 + j))
+            accs.append(lone[:])
+        for e in range(E):
+            for o in range(PASSES):
+                product(e, accs[e], o)
 
-        def gather_last(experts, tag):
-            words = keep.tile([P, len(experts), C], U32, name="last%d" % experts[0], tag=tag, align_bytes=64)
-            for j, e in enumerate(experts):
-                last_words[e] = words[:, j, :]
-                nc.vector.tensor_copy(
-                    words[:, j, :], xw[PASSES - 1][:].bitcast(U32).indirect(offs_sb[:, e * C // 16 : (e + 1) * C // 16])
-                )
+        y = keep.tile([P, S], F32, name="y", tag="raw%d" % E, align_bytes=64)
+        for e in range(E):
+            nc.scalar.activation(out=y[:, e * C : (e + 1) * C], in_=accs[e], func=IDENT, bias=bias[:, e : e + 1])
 
-        first = E - GROUP
-        for e in range(first, E):
-            cast(e)
-            quantize(e)
-            if e == first:
-                gather_scales(GROUPS - 1, "raw%d_%d" % (e, PASSES))
-            else:
-                gather_last([e - 1] if e < E - 1 else [e - 1, e], "raw%d_%d" % (e, PASSES))
-
-        y = keep.tile([P, S], F32, name="y", tag="raw%d_%d" % (E - 1, PASSES - 1), align_bytes=64)
-
-        def empty_scalar(e, acc):
-            nc.scalar.activation(out=y[:, e * C : (e + 1) * C], in_=acc, func=IDENT, bias=bias[:, e : e + 1])
-
-        for e in range(E - GROUP):
-            empty_scalar(e, pairs[e // 2][:, e % 2, :])
-
-        cast(E)
-
-        first = E - GROUP
-        accs = [psum.tile([P, C], F32, name="acc%d" % j, tag="bank%d" % (4 + j)) for j in range(GROUP)]
-        for o in range(PASSES - 1):
-            for j in range(GROUP):
-                product(first + j, accs[j][:], o)
-        for j in range(GROUP):
-            e = first + j
-            product(e, accs[j][:], PASSES - 1)
-            empty_scalar(e, accs[j][:])
-
-        quantize(E)
         shared_banks = []
         for c in range(T // BANK):
             acc = psum.tile([P, BANK], F32, name="shared%d" % c, tag="bank%d" % c)
@@ -207,7 +179,7 @@ def tile_moe_shr_lin_bias_kernel(tc, x_words, x_scales, w, b, gate, offs, pos1, 
                     stop=(o == PASSES - 1),
                 )
 
-        shared = keep.tile([P, turned_end], F32, name="shared", tag="raw0_%d" % PASSES, align_bytes=64)
+        shared = keep.tile([P, turned_end], F32, name="shared", tag="raw0", align_bytes=64)
         for c in range(T // BANK):
             lo, hi = c * BANK, min(turned_end, (c + 1) * BANK)
             if hi > lo:
@@ -216,7 +188,7 @@ def tile_moe_shr_lin_bias_kernel(tc, x_words, x_scales, w, b, gate, offs, pos1, 
                 )
 
         def pick(i, lo, hi):
-            picked = keep.tile([P, hi - lo], F32, name="pick%d_%d" % (i, lo))
+            picked = keep.tile([P, hi - lo], F32, name="pick%d_%d" % (i, lo), tag="raw%d" % (1 + 2 * edges.index(lo) + i), align_bytes=64)
             nc.vector.tensor_tensor(
                 picked[:], y[:].indirect(pos_sb[i][:, lo // 16 : hi // 16]), gates[i][:, lo:hi], MULT
             )

@@ -146,15 +146,15 @@ def tile_moe_shr_lin_bias_kernel(tc, x_words, x_scales, w, b, gate, offs, pos1, 
         for g in range(GROUPS - 1):
             gather_words(g, 2, "gw%d_2" % g, whole)
         quantize(*sets[4])
-        gather_words(GROUPS - 1, 2, "raw%d" % (E - 1), [(0, 2 * C), (2 * C, 3 * C), (3 * C, 4 * C)])
+        gather_words(GROUPS - 1, 2, "raw%d" % (E - 1), [(j * C, (j + 1) * C) for j in range(GROUP)])
         quantize(*sets[5])
 
         accs = []
-        for h in range(E // 2 - 1):
+        for h in range((E - GROUP) // 2):
             pair = psum.tile([P, 2, C], F32, name="pair%d" % h, tag="bank%d" % h)
             accs.extend([pair[:, 0, :], pair[:, 1, :]])
-        for j in range(2):
-            lone = psum.tile([P, C], F32, name="lone%d" % j, tag="bank%d" % (E // 2 - 1 + j))
+        for j in range(GROUP):
+            lone = psum.tile([P, C], F32, name="lone%d" % j, tag="bank%d" % ((E - GROUP) // 2 + j))
             accs.append(lone[:])
         for e in range(E):
             for o in range(PASSES):
@@ -187,8 +187,11 @@ def tile_moe_shr_lin_bias_kernel(tc, x_words, x_scales, w, b, gate, offs, pos1, 
                     out=shared[:, lo:hi], in_=shared_banks[c][:, 0 : hi - lo], func=IDENT, bias=bias[:, E : E + 1]
                 )
 
+        picks = []
+
         def pick(i, lo, hi):
-            picked = keep.tile([P, hi - lo], F32, name="pick%d_%d" % (i, lo), tag="raw%d" % (1 + 2 * edges.index(lo) + i), align_bytes=64)
+            picked = keep.tile([P, hi - lo], F32, name="pick%d_%d" % (i, lo), tag="raw%d" % (1 + len(picks)), align_bytes=64)
+            picks.append(picked)
             nc.vector.tensor_tensor(
                 picked[:], y[:].indirect(pos_sb[i][:, lo // 16 : hi // 16]), gates[i][:, lo:hi], MULT
             )
@@ -217,12 +220,15 @@ def tile_moe_shr_lin_bias_kernel(tc, x_words, x_scales, w, b, gate, offs, pos1, 
             nc.sync.dma_start(out=out[:, lo:hi], in_=res[:])
 
         lo, hi = chunks[-1]
+        mid = hi - P
         first_pick = pick(0, lo, hi)
-        second_pick = pick(1, lo, hi)
+        second_picks = [pick(1, lo, mid)]
         part = keep.tile([P, hi - lo], F32, name="part")
         nc.vector.scalar_tensor_tensor(
             out=part[:], in0=shared_banks[lo // BANK][:, lo % BANK : BANK], scalar=bias[:, E : E + 1], in1=first_pick[:], op0=ADD, op1=ADD
         )
-        res = keep.tile([P, hi - lo], F32, name="res_last")
-        nc.vector.tensor_tensor(res[:], part[:], second_pick[:], ADD)
-        nc.sync.dma_start(out=out[:, lo:hi], in_=res[:])
+        second_picks.append(pick(1, mid, hi))
+        for second_pick, (a, z) in zip(second_picks, ((lo, mid), (mid, hi))):
+            res = keep.tile([P, z - a], F32, name="res_last%d" % a)
+            nc.vector.tensor_tensor(res[:], part[:, a - lo : z - lo], second_pick[:], ADD)
+            nc.sync.dma_start(out=out[:, a:z], in_=res[:])

@@ -24,6 +24,7 @@ GROUP = 4
 GROUPS = E // GROUP
 GSLOTS = GROUP * C
 BANK = 512
+WINDOW = 2048
 
 
 def tile_moe_shr_lin_bias_kernel(tc, x_words, x_scales, w, b, gate, offs, pos1, pos2, out):
@@ -35,12 +36,12 @@ def tile_moe_shr_lin_bias_kernel(tc, x_words, x_scales, w, b, gate, offs, pos1, 
         edges = (0, 512, 896, 1152, 1536)
         chunks = list(zip(edges[:-1], edges[1:]))
         turned_end = edges[-2]
-        sets = ((0, 2), (2, 6), (6, 10), (10, 11), (11, 12), (12, 13))
+        sets = ((0, 8), (8, 12), (12, 13))
 
         offs_sb = keep.tile([P, S // 16], U16, name="offs_sb")
         pos_sb = [keep.tile([P, T // 16], U16, name="pos%d" % i) for i in range(2)]
-        xw = [keep.tile([P, T], I32, name="xw%d" % o, align_bytes=64) for o in range(PASSES)]
-        xs = keep.tile([P, T], U8, name="xs", align_bytes=64)
+        xw = [keep.tile([P, WINDOW if o < PASSES - 1 else T], I32, name="xw%d" % o, align_bytes=64) for o in range(PASSES)]
+        xs = keep.tile([P, WINDOW], U8, name="xs", align_bytes=64)
         bias = keep.tile([P, E + 1], F32, name="bias")
         gates = [keep.tile([P, T], F32, name="gate%d" % i) for i in range(2)]
         ident = keep.tile([P, P], F32, name="ident")
@@ -50,16 +51,18 @@ def tile_moe_shr_lin_bias_kernel(tc, x_words, x_scales, w, b, gate, offs, pos1, 
             nc.sync.dma_start(out=raw[e][:], in_=w[e].rearrange("(o p r) n -> p o r n", o=PASSES, r=4))
 
         def load_x(o):
-            nc.sync.dma_start(out=xw[o][:], in_=x_words[o].rearrange("p t r -> p (t r)").bitcast(I32))
+            nc.sync.dma_start(out=xw[o][:, 0:T], in_=x_words[o].rearrange("p t r -> p (t r)").bitcast(I32))
 
         def load_scales():
             for q in range(4):
                 nc.sync.dma_start(
-                    out=xs[32 * q : 32 * q + 4 * PASSES, :].bitcast(I32),
+                    out=xs[32 * q : 32 * q + 4 * PASSES, 0:T].bitcast(I32),
                     in_=x_scales[:, 4 * q : 4 * q + 4, :].bitcast(I32),
                 )
 
         nc.vector.memset(xs[:].bitcast(I32), 0)
+        for o in range(PASSES - 1):
+            nc.gpsimd.memset(xw[o][:, T:WINDOW], 0)
         make_identity(nc, ident[:])
         load_x(0)
         nc.sync.dma_start(offs_sb[:], offs)
@@ -69,10 +72,10 @@ def tile_moe_shr_lin_bias_kernel(tc, x_words, x_scales, w, b, gate, offs, pos1, 
         for e in range(1, 6):
             load_w(e)
         load_x(1)
-        for e in range(6, 11):
+        for e in range(6, 10):
             load_w(e)
         load_x(2)
-        for e in range(11, E + 1):
+        for e in range(10, E + 1):
             load_w(e)
         nc.sync.dma_start(pos_sb[0][:], pos1)
         nc.sync.dma_start(pos_sb[1][:], pos2)
@@ -105,64 +108,66 @@ def tile_moe_shr_lin_bias_kernel(tc, x_words, x_scales, w, b, gate, offs, pos1, 
                     )
                     lo = lo + width
 
-        gw = {}
-        gs = {}
+        late = S - GSLOTS
+        gw = [keep.tile([P, S if o < PASSES - 1 else late], U32, name="gw%d" % o, align_bytes=64) for o in range(PASSES)]
+        gs = keep.tile([P, S], U8, name="gs", align_bytes=64)
 
-        def gather_words(g, o, tag, cuts):
-            gw[g, o] = keep.tile([P, GSLOTS], U32, name="gw%d_%d" % (g, o), tag=tag, align_bytes=64)
-            for lo, hi in cuts:
-                nc.vector.tensor_copy(
-                    gw[g, o][:, lo:hi],
-                    xw[o][:].bitcast(U32).indirect(offs_sb[:, (g * GSLOTS + lo) // 16 : (g * GSLOTS + hi) // 16]),
-                )
+        def gather(dst, window, lo, hi):
+            nc.vector.tensor_copy(dst, window.indirect(offs_sb[:, lo // 16 : hi // 16]))
 
-        def gather_scales(g):
-            gs[g] = keep.tile([P, GSLOTS], U8, name="gs%d" % g, align_bytes=64)
-            nc.vector.tensor_copy(gs[g][:], xs[:].indirect(offs_sb[:, g * GSLOTS // 16 : (g + 1) * GSLOTS // 16]))
+        halves = ((0, S // 2), (S // 2, S))
+        for lo, hi in halves:
+            gather(gw[0][:, lo:hi], xw[0][:].bitcast(U32), lo, hi)
+        for lo, hi in halves:
+            gather(gs[:, lo:hi], xs[:], lo, hi)
+        for lo, hi in halves:
+            gather(gw[1][:, lo:hi], xw[1][:].bitcast(U32), lo, hi)
+        quantize(*sets[0])
+        for lo in range(0, late, GSLOTS):
+            gather(gw[2][:, lo : lo + GSLOTS], xw[2][:].bitcast(U32), lo, lo + GSLOTS)
+        quantize(*sets[1])
+        last = keep.tile([P, GSLOTS], U32, name="last", tag="raw%d" % (E - 1), align_bytes=64)
+        for lo, hi in ((0, 2 * C), (2 * C, 3 * C), (3 * C, 4 * C)):
+            gather(last[:, lo:hi], xw[2][:].bitcast(U32), late + lo, late + hi)
+        quantize(*sets[2])
 
-        def product(e, acc, o):
-            g, j = divmod(e, GROUP)
+        def product(acc, o, lo, hi, start, stop):
+            e = lo // C
+            words = last[:, lo - late : hi - late] if (o == PASSES - 1 and lo >= late) else gw[o][:, lo:hi]
             nc.tensor.matmul_mx(
                 out=acc,
                 lhsT=wq[e][:, o * N : (o + 1) * N].bitcast(FP8X4),
                 lhsT_scale=ws[e][:, o * N : (o + 1) * N],
-                rhs=gw[g, o][:, j * C : (j + 1) * C].bitcast(FP8X4),
-                rhs_scale=gs[g][4 * o : P, j * C : (j + 1) * C],
-                start=(o == 0),
-                stop=(o == PASSES - 1),
+                rhs=words.bitcast(FP8X4),
+                rhs_scale=gs[4 * o : P, lo:hi],
+                start=start,
+                stop=stop,
             )
 
-        whole = [(0, GSLOTS)]
-        for g in range(GROUPS):
-            gather_words(g, 0, "gw%d_0" % g, whole)
-        for g in range(GROUPS):
-            gather_scales(g)
-        quantize(*sets[0])
-        quantize(*sets[1])
-        for g in range(GROUPS):
-            gather_words(g, 1, "gw%d_1" % g, whole)
-        quantize(*sets[2])
-        quantize(*sets[3])
-        for g in range(GROUPS - 1):
-            gather_words(g, 2, "gw%d_2" % g, whole)
-        quantize(*sets[4])
-        gather_words(GROUPS - 1, 2, "raw%d" % (E - 1), [(j * C, (j + 1) * C) for j in range(GROUP)])
-        quantize(*sets[5])
-
         accs = []
-        for h in range((E - GROUP) // 2):
+        for h in range(E // 2 - 1):
             pair = psum.tile([P, 2, C], F32, name="pair%d" % h, tag="bank%d" % h)
             accs.extend([pair[:, 0, :], pair[:, 1, :]])
-        for j in range(GROUP):
-            lone = psum.tile([P, C], F32, name="lone%d" % j, tag="bank%d" % ((E - GROUP) // 2 + j))
-            accs.append(lone[:])
-        for e in range(E):
+        lone = psum.tile([P, C], F32, name="lone", tag="bank%d" % (E // 2 - 1))
+        accs.append(lone[:])
+        ends = [psum.tile([P, P], F32, name="end%d" % j, tag="bank%d" % (E // 2 + j)) for j in range(2)]
+        for e in range(E - GROUP):
             for o in range(PASSES):
-                product(e, accs[e], o)
+                product(accs[e], o, e * C, (e + 1) * C, o == 0, o == PASSES - 1)
+        for o in range(PASSES):
+            for e in (E - GROUP, E - GROUP + 1):
+                product(accs[e], o, e * C, (e + 1) * C, o == 0 and e == E - GROUP, o == PASSES - 1 and e > E - GROUP)
+        for o in range(PASSES):
+            product(accs[E - 2], o, S - 2 * C, S - C, o == 0, o == PASSES - 1)
+        for j in range(2):
+            for o in range(PASSES):
+                product(ends[j][:], o, S - C + j * P, S - C + (j + 1) * P, o == 0, o == PASSES - 1)
 
         y = keep.tile([P, S], F32, name="y", tag="raw%d" % E, align_bytes=64)
-        for e in range(E):
+        for e in range(E - 1):
             nc.scalar.activation(out=y[:, e * C : (e + 1) * C], in_=accs[e], func=IDENT, bias=bias[:, e : e + 1])
+        nc.scalar.activation(out=y[:, S - C : S - P], in_=ends[0][:], func=IDENT, bias=bias[:, E - 1 : E])
+        nc.vector.tensor_scalar_add(y[:, S - P : S], ends[1][:], bias[:, E - 1 : E])
 
         shared_banks = []
         for c in range(T // BANK):

@@ -67,9 +67,10 @@ def tile_moe_shr_lin_bias_kernel(tc, x_words, x_scales, w, b, gate, offs, pos1, 
         load_x(0)
         nc.sync.dma_start(offs_sb[:], offs)
         load_w(0)
-        nc.sync.dma_start(bias[:], b)
+        load_w(1)
         load_scales()
-        for e in range(1, 6):
+        nc.sync.dma_start(bias[:], b)
+        for e in range(2, 6):
             load_w(e)
         load_x(1)
         for e in range(6, 10):
@@ -204,17 +205,29 @@ def tile_moe_shr_lin_bias_kernel(tc, x_words, x_scales, w, b, gate, offs, pos1, 
 
         sum_banks = (3, 4, 5)
         back_banks = (6, 7, 0)
+        totals = [
+            psum.tile([P, hi - lo], F32, name="total%d" % c, tag="bank%d" % sum_banks[c])
+            for c, (lo, hi) in enumerate(chunks[:-1])
+        ]
+
+        def turn_onto(c, term, start, stop):
+            blocks = (chunks[c][1] - chunks[c][0]) // P
+            for k in range(blocks):
+                nc.tensor.matmul(
+                    totals[c][:, k * P : (k + 1) * P], term[:, k * P : (k + 1) * P], ident[:], is_transpose=True,
+                    start=(start and k == 0), stop=(stop and k == blocks - 1),
+                )
+
+        early_pick = pick(0, 0, turned_end)
+        for c, (lo, hi) in enumerate(chunks[:-1]):
+            turn_onto(c, shared[:, lo:hi], True, False)
+        for c, (lo, hi) in enumerate(chunks[:-1]):
+            turn_onto(c, early_pick[:, lo:hi], False, False)
         for c, (lo, hi) in enumerate(chunks[:-1]):
             width = hi - lo
-            terms = [shared[:, lo:hi], pick(0, lo, hi)[:], pick(1, lo, hi)[:]]
             blocks = width // P
-            total = psum.tile([P, width], F32, name="total%d" % c, tag="bank%d" % sum_banks[c])
-            for i, term in enumerate(terms):
-                for k in range(blocks):
-                    nc.tensor.matmul(
-                        total[:, k * P : (k + 1) * P], term[:, k * P : (k + 1) * P], ident[:], is_transpose=True,
-                        start=(i == 0 and k == 0), stop=(i == 2 and k == blocks - 1),
-                    )
+            total = totals[c]
+            turn_onto(c, pick(1, lo, hi)[:], False, True)
             turned = keep.tile([P, width], F32, name="turned%d" % c)
             nc.scalar.copy(out=turned[:], in_=total[:])
             back = psum.tile([P, width], F32, name="back%d" % c, tag="bank%d" % back_banks[c])

@@ -33,9 +33,8 @@ def tile_moe_shr_lin_bias_kernel(tc, x_words, x_scales, w, b, gate, offs, pos1, 
         keep = ctx.enter_context(tc.tile_pool(name="keep", bufs=1))
         psum = ctx.enter_context(tc.psum_pool(name="psum", bufs=1))
 
-        edges = (0, 512, 896, 1152, 1536)
+        edges = (0, 512, 896, 1024, 1536)
         chunks = list(zip(edges[:-1], edges[1:]))
-        turned_end = edges[-2]
         sets = ((0, 8), (8, 12), (12, 13))
 
         offs_sb = keep.tile([P, S // 16], U16, name="offs_sb")
@@ -185,13 +184,10 @@ def tile_moe_shr_lin_bias_kernel(tc, x_words, x_scales, w, b, gate, offs, pos1, 
                     stop=(o == PASSES - 1),
                 )
 
-        shared = keep.tile([P, turned_end], F32, name="shared", tag="raw0", align_bytes=64)
+        shared = keep.tile([P, T], F32, name="shared", tag="raw0", align_bytes=64)
         for c in range(T // BANK):
-            lo, hi = c * BANK, min(turned_end, (c + 1) * BANK)
-            if hi > lo:
-                nc.scalar.activation(
-                    out=shared[:, lo:hi], in_=shared_banks[c][:, 0 : hi - lo], func=IDENT, bias=bias[:, E : E + 1]
-                )
+            lo, hi = c * BANK, (c + 1) * BANK
+            nc.scalar.activation(out=shared[:, lo:hi], in_=shared_banks[c][:], func=IDENT, bias=bias[:, E : E + 1])
 
         picks = []
 
@@ -203,11 +199,11 @@ def tile_moe_shr_lin_bias_kernel(tc, x_words, x_scales, w, b, gate, offs, pos1, 
             )
             return picked
 
-        sum_banks = (3, 4, 5)
-        back_banks = (6, 7, 0)
+        sum_banks = (3, 4, 5, 6)
+        back_banks = (7, 1, 2, 0)
         totals = [
             psum.tile([P, hi - lo], F32, name="total%d" % c, tag="bank%d" % sum_banks[c])
-            for c, (lo, hi) in enumerate(chunks[:-1])
+            for c, (lo, hi) in enumerate(chunks)
         ]
 
         def turn_onto(c, term, start, stop):
@@ -218,35 +214,44 @@ def tile_moe_shr_lin_bias_kernel(tc, x_words, x_scales, w, b, gate, offs, pos1, 
                     start=(start and k == 0), stop=(stop and k == blocks - 1),
                 )
 
-        early_pick = pick(0, 0, turned_end)
-        for c, (lo, hi) in enumerate(chunks[:-1]):
-            turn_onto(c, shared[:, lo:hi], True, False)
-        for c, (lo, hi) in enumerate(chunks[:-1]):
-            turn_onto(c, early_pick[:, lo:hi], False, False)
-        for c, (lo, hi) in enumerate(chunks[:-1]):
-            width = hi - lo
-            blocks = width // P
-            total = totals[c]
-            turn_onto(c, pick(1, lo, hi)[:], False, True)
+        def turn_back(c):
+            width = chunks[c][1] - chunks[c][0]
             turned = keep.tile([P, width], F32, name="turned%d" % c)
-            nc.scalar.copy(out=turned[:], in_=total[:])
+            nc.scalar.copy(out=turned[:], in_=totals[c][:])
             back = psum.tile([P, width], F32, name="back%d" % c, tag="bank%d" % back_banks[c])
-            for k in range(blocks):
+            for k in range(width // P):
                 nc.tensor.transpose(back[:, k * P : (k + 1) * P], turned[:, k * P : (k + 1) * P], ident[:])
-            res = keep.tile([P, width], F32, name="res%d" % c)
+            return back
+
+        def store(c, back):
+            lo, hi = chunks[c]
+            res = keep.tile([P, hi - lo], F32, name="res%d" % c)
             nc.scalar.copy(out=res[:], in_=back[:])
             nc.sync.dma_start(out=out[:, lo:hi], in_=res[:])
 
-        lo, hi = chunks[-1]
-        mid = hi - P
-        first_pick = pick(0, lo, hi)
-        second_picks = [pick(1, lo, mid)]
-        part = keep.tile([P, hi - lo], F32, name="part")
-        nc.vector.scalar_tensor_tensor(
-            out=part[:], in0=shared_banks[lo // BANK][:, lo % BANK : BANK], scalar=bias[:, E : E + 1], in1=first_pick[:], op0=ADD, op1=ADD
-        )
-        second_picks.append(pick(1, mid, hi))
-        for second_pick, (a, z) in zip(second_picks, ((lo, mid), (mid, hi))):
+        mixed = len(chunks) - 1
+        lo, hi = chunks[0]
+        turn_onto(0, shared[:, lo:hi], True, False)
+        turn_onto(0, pick(0, lo, hi)[:], False, False)
+        turn_onto(0, pick(1, lo, hi)[:], False, True)
+        store(0, turn_back(0))
+
+        rest = hi
+        first_pick = pick(0, rest, T)
+        order = [mixed] + list(range(1, mixed))
+        for c in order:
+            turn_onto(c, shared[:, edges[c] : edges[c + 1]], True, False)
+        for c in order:
+            turn_onto(c, first_pick[:, edges[c] - rest : edges[c + 1] - rest], False, c == mixed)
+        part = turn_back(mixed)
+        for c in range(1, mixed):
+            turn_onto(c, pick(1, *chunks[c])[:], False, True)
+            store(c, turn_back(c))
+
+        lo, hi = chunks[mixed]
+        ranges = ((lo, hi - P), (hi - P, hi))
+        second_picks = [pick(1, a, z) for a, z in ranges]
+        for second_pick, (a, z) in zip(second_picks, ranges):
             res = keep.tile([P, z - a], F32, name="res_last%d" % a)
             nc.vector.tensor_tensor(res[:], part[:, a - lo : z - lo], second_pick[:], ADD)
             nc.sync.dma_start(out=out[:, a:z], in_=res[:])

@@ -33,7 +33,7 @@ def tile_moe_shr_lin_bias_kernel(tc, x_words, x_scales, w, b, gate, offs, pos1, 
         keep = ctx.enter_context(tc.tile_pool(name="keep", bufs=1))
         psum = ctx.enter_context(tc.psum_pool(name="psum", bufs=1))
 
-        edges = (0, 512, 896, 1024, 1536)
+        edges = (0, 512, 896, 1280, 1536)
         chunks = list(zip(edges[:-1], edges[1:]))
         sets = ((0, 8), (8, 12), (12, 13))
 
@@ -200,7 +200,7 @@ def tile_moe_shr_lin_bias_kernel(tc, x_words, x_scales, w, b, gate, offs, pos1, 
             return picked
 
         sum_banks = (3, 4, 5, 6)
-        back_banks = (7, 1, 2, 0)
+        back_banks = (7, 1, 0, 2)
         totals = [
             psum.tile([P, hi - lo], F32, name="total%d" % c, tag="bank%d" % sum_banks[c])
             for c, (lo, hi) in enumerate(chunks)
@@ -229,29 +229,27 @@ def tile_moe_shr_lin_bias_kernel(tc, x_words, x_scales, w, b, gate, offs, pos1, 
             nc.scalar.copy(out=res[:], in_=back[:])
             nc.sync.dma_start(out=out[:, lo:hi], in_=res[:])
 
-        mixed = len(chunks) - 1
         lo, hi = chunks[0]
         turn_onto(0, shared[:, lo:hi], True, False)
         turn_onto(0, pick(0, lo, hi)[:], False, False)
         turn_onto(0, pick(1, lo, hi)[:], False, True)
         store(0, turn_back(0))
 
-        rest = hi
-        first_pick = pick(0, rest, T)
-        order = [mixed] + list(range(1, mixed))
-        for c in order:
+        first_pick = pick(0, edges[1], edges[3])
+        for c in (2, 1, 3):
             turn_onto(c, shared[:, edges[c] : edges[c + 1]], True, False)
-        for c in order:
-            turn_onto(c, first_pick[:, edges[c] - rest : edges[c + 1] - rest], False, c == mixed)
-        part = turn_back(mixed)
-        for c in range(1, mixed):
-            turn_onto(c, pick(1, *chunks[c])[:], False, True)
-            store(c, turn_back(c))
+        for c in (2, 1):
+            turn_onto(c, first_pick[:, edges[c] - edges[1] : edges[c + 1] - edges[1]], False, c == 2)
+        parts = {2: turn_back(2)}
+        turn_onto(1, pick(1, *chunks[1])[:], False, True)
+        back = turn_back(1)
+        turn_onto(3, pick(0, *chunks[3])[:], False, True)
+        parts[3] = turn_back(3)
+        store(1, back)
 
-        lo, hi = chunks[mixed]
-        ranges = ((lo, hi - P), (hi - P, hi))
-        second_picks = [pick(1, a, z) for a, z in ranges]
-        for second_pick, (a, z) in zip(second_picks, ranges):
-            res = keep.tile([P, z - a], F32, name="res_last%d" % a)
-            nc.vector.tensor_tensor(res[:], part[:, a - lo : z - lo], second_pick[:], ADD)
-            nc.sync.dma_start(out=out[:, a:z], in_=res[:])
+        second_picks = {c: pick(1, *chunks[c]) for c in (2, 3)}
+        for c in (2, 3):
+            lo, hi = chunks[c]
+            res = keep.tile([P, hi - lo], F32, name="res%d" % c)
+            nc.vector.tensor_tensor(res[:], parts[c][:], second_picks[c][:], ADD)
+            nc.sync.dma_start(out=out[:, lo:hi], in_=res[:])

@@ -214,10 +214,13 @@ def tile_moe_shr_lin_bias_kernel(tc, x_words, x_scales, w, b, gate, offs, pos1, 
                     start=(start and k == 0), stop=(stop and k == blocks - 1),
                 )
 
-        def turn_back(c):
-            width = chunks[c][1] - chunks[c][0]
-            turned = keep.tile([P, width], F32, name="turned%d" % c)
+        def empty(c):
+            turned = keep.tile([P, chunks[c][1] - chunks[c][0]], F32, name="turned%d" % c)
             nc.scalar.copy(out=turned[:], in_=totals[c][:])
+            return turned
+
+        def turn_back(c, turned):
+            width = chunks[c][1] - chunks[c][0]
             back = psum.tile([P, width], F32, name="back%d" % c, tag="bank%d" % back_banks[c])
             for k in range(width // P):
                 nc.tensor.transpose(back[:, k * P : (k + 1) * P], turned[:, k * P : (k + 1) * P], ident[:])
@@ -233,23 +236,22 @@ def tile_moe_shr_lin_bias_kernel(tc, x_words, x_scales, w, b, gate, offs, pos1, 
         turn_onto(0, shared[:, lo:hi], True, False)
         turn_onto(0, pick(0, lo, hi)[:], False, False)
         turn_onto(0, pick(1, lo, hi)[:], False, True)
-        store(0, turn_back(0))
+        store(0, turn_back(0, empty(0)))
 
         first_pick = pick(0, edges[1], edges[3])
         for c in (2, 1, 3):
             turn_onto(c, shared[:, edges[c] : edges[c + 1]], True, False)
         for c in (2, 1):
             turn_onto(c, first_pick[:, edges[c] - edges[1] : edges[c + 1] - edges[1]], False, c == 2)
-        parts = {2: turn_back(2)}
         turn_onto(1, pick(1, *chunks[1])[:], False, True)
-        back = turn_back(1)
         turn_onto(3, pick(0, *chunks[3])[:], False, True)
-        parts[3] = turn_back(3)
-        store(1, back)
+        turned = {c: empty(c) for c in (2, 1, 3)}
+        backs = {c: turn_back(c, turned[c]) for c in (2, 1, 3)}
+        store(1, backs[1])
 
         second_picks = {c: pick(1, *chunks[c]) for c in (2, 3)}
         for c in (2, 3):
             lo, hi = chunks[c]
             res = keep.tile([P, hi - lo], F32, name="res%d" % c)
-            nc.vector.tensor_tensor(res[:], parts[c][:], second_picks[c][:], ADD)
+            nc.vector.tensor_tensor(res[:], backs[c][:], second_picks[c][:], ADD)
             nc.sync.dma_start(out=out[:, lo:hi], in_=res[:])

@@ -33,7 +33,7 @@ def tile_moe_shr_lin_bias_kernel(tc, x_words, x_scales, w, b, gate, offs, pos1, 
         keep = ctx.enter_context(tc.tile_pool(name="keep", bufs=1))
         psum = ctx.enter_context(tc.psum_pool(name="psum", bufs=1))
 
-        edges = (0, 512, 896, 1280, 1536)
+        edges = (0, 512, 768, 1024, 1280, 1536)
         chunks = list(zip(edges[:-1], edges[1:]))
         sets = ((0, 8), (8, 12), (12, 13))
 
@@ -167,7 +167,7 @@ def tile_moe_shr_lin_bias_kernel(tc, x_words, x_scales, w, b, gate, offs, pos1, 
         for e in range(E - 1):
             nc.scalar.activation(out=y[:, e * C : (e + 1) * C], in_=accs[e], func=IDENT, bias=bias[:, e : e + 1])
         nc.scalar.activation(out=y[:, S - C : S - P], in_=ends[0][:], func=IDENT, bias=bias[:, E - 1 : E])
-        nc.vector.tensor_scalar_add(y[:, S - P : S], ends[1][:], bias[:, E - 1 : E])
+        nc.scalar.activation(out=y[:, S - P : S], in_=ends[1][:], func=IDENT, bias=bias[:, E - 1 : E])
 
         shared_banks = []
         for c in range(T // BANK):
@@ -199,8 +199,8 @@ def tile_moe_shr_lin_bias_kernel(tc, x_words, x_scales, w, b, gate, offs, pos1, 
             )
             return picked
 
-        sum_banks = (3, 4, 5, 6)
-        back_banks = (7, 1, 0, 2)
+        sum_banks = (3, 4, 5, 6, 7)
+        back_banks = (0, 1, 2, 3, 4)
         totals = [
             psum.tile([P, hi - lo], F32, name="total%d" % c, tag="bank%d" % sum_banks[c])
             for c, (lo, hi) in enumerate(chunks)
@@ -238,20 +238,21 @@ def tile_moe_shr_lin_bias_kernel(tc, x_words, x_scales, w, b, gate, offs, pos1, 
         turn_onto(0, pick(1, lo, hi)[:], False, True)
         store(0, turn_back(0, empty(0)))
 
-        first_pick = pick(0, edges[1], edges[3])
-        for c in (2, 1, 3):
+        first_pick = pick(0, edges[1], edges[4])
+        for c in (1, 2, 3, 4):
             turn_onto(c, shared[:, edges[c] : edges[c + 1]], True, False)
-        for c in (2, 1):
-            turn_onto(c, first_pick[:, edges[c] - edges[1] : edges[c + 1] - edges[1]], False, c == 2)
+        for c in (1, 2, 3):
+            turn_onto(c, first_pick[:, edges[c] - edges[1] : edges[c + 1] - edges[1]], False, c > 1)
         turn_onto(1, pick(1, *chunks[1])[:], False, True)
-        turn_onto(3, pick(0, *chunks[3])[:], False, True)
-        turned = {c: empty(c) for c in (2, 1, 3)}
-        backs = {c: turn_back(c, turned[c]) for c in (2, 1, 3)}
+        turn_onto(4, pick(0, *chunks[4])[:], False, True)
+        turned = {c: empty(c) for c in (1, 2, 3, 4)}
+        backs = {c: turn_back(c, turned[c]) for c in (1, 2, 3, 4)}
         store(1, backs[1])
 
-        second_picks = {c: pick(1, *chunks[c]) for c in (2, 3)}
-        for c in (2, 3):
+        wide = pick(1, edges[2], edges[4])
+        second_picks = {2: wide[:, 0:C], 3: wide[:, C : 2 * C], 4: pick(1, *chunks[4])[:]}
+        for c in (2, 3, 4):
             lo, hi = chunks[c]
             res = keep.tile([P, hi - lo], F32, name="res%d" % c)
-            nc.vector.tensor_tensor(res[:], backs[c][:], second_picks[c][:], ADD)
+            nc.vector.tensor_tensor(res[:], backs[c][:], second_picks[c], ADD)
             nc.sync.dma_start(out=out[:, lo:hi], in_=res[:])

@@ -40,9 +40,11 @@ def tile_moe_shr_lin_bias_kernel(tc, x_words, x_scales, w, b, gate, offs, pos1, 
         offs_sb = keep.tile([P, S // 16], U16, name="offs_sb")
         pos_sb = [keep.tile([P, T // 16], U16, name="pos%d" % i) for i in range(2)]
         xw = [keep.tile([P, WINDOW if o < PASSES - 1 else T], I32, name="xw%d" % o, align_bytes=64) for o in range(PASSES)]
-        xs = keep.tile([P, WINDOW], U8, name="xs", align_bytes=64)
+        xs = keep.tile([P, 2 * WINDOW], U8, name="xs", align_bytes=64)
+        rows = keep.tile([P, T], U8, name="rows", align_bytes=64)
+        late_scales = keep.tile([P, GSLOTS], U8, name="late_scales", align_bytes=64)
+        home = (0, 16, 80)
         bias = keep.tile([P, E + 1], F32, name="bias")
-        gates = [keep.tile([P, T], F32, name="gate%d" % i) for i in range(2)]
         ident = keep.tile([P, P], F32, name="ident")
         raw = [keep.tile([P, PASSES, 4, N], F32, name="raw%d" % e, align_bytes=64) for e in range(E + 1)]
 
@@ -59,12 +61,19 @@ def tile_moe_shr_lin_bias_kernel(tc, x_words, x_scales, w, b, gate, offs, pos1, 
                     in_=x_scales[:, 4 * q : 4 * q + 4, :].bitcast(I32),
                 )
 
-        nc.vector.memset(xs[:].bitcast(I32), 0)
+        all_rows = x_scales.rearrange("o f t -> (o f) t").bitcast(I32)
+        nc.vector.memset(xs[:, 0:T].bitcast(I32), 0)
+        nc.vector.memset(xs[:, T:].bitcast(I32), 0)
+        nc.gpsimd.memset(rows[32:64, :].bitcast(I32), 0)
+        nc.gpsimd.memset(rows[96:P, :].bitcast(I32), 0)
         for o in range(PASSES - 1):
             nc.gpsimd.memset(xw[o][:, T:WINDOW], 0)
+        nc.gpsimd.memset(late_scales[:].bitcast(I32), 0)
         make_identity(nc, ident[:])
-        load_x(0)
         nc.sync.dma_start(offs_sb[:], offs)
+        nc.sync.dma_start(out=rows[0:32, :].bitcast(I32), in_=all_rows[0:32])
+        nc.sync.dma_start(out=rows[64:96, :].bitcast(I32), in_=all_rows[16:48])
+        load_x(0)
         load_w(0)
         load_w(1)
         load_scales()
@@ -72,15 +81,13 @@ def tile_moe_shr_lin_bias_kernel(tc, x_words, x_scales, w, b, gate, offs, pos1, 
         for e in range(2, 6):
             load_w(e)
         load_x(1)
+        nc.sync.dma_start(pos_sb[0][:], pos1)
+        nc.sync.dma_start(pos_sb[1][:], pos2)
         for e in range(6, 10):
             load_w(e)
         load_x(2)
         for e in range(10, E + 1):
             load_w(e)
-        nc.sync.dma_start(pos_sb[0][:], pos1)
-        nc.sync.dma_start(pos_sb[1][:], pos2)
-        for i in range(2):
-            nc.sync.dma_start(gates[i][:], gate[i])
 
         wq = {}
         ws = {}
@@ -89,7 +96,7 @@ def tile_moe_shr_lin_bias_kernel(tc, x_words, x_scales, w, b, gate, offs, pos1, 
             words = (end - first) * PASSES * N
             stage = keep.tile([P, 4 * words], BF16, name="stage%d" % first, align_bytes=64)
             codes = keep.tile([P, words], U32, name="wq%d" % first, align_bytes=64)
-            scales = keep.tile([P, words], U8, name="ws%d" % first, align_bytes=64)
+            scales = keep.tile([P, words], U8, name="ws%d" % first, tag="grows" if first == E else "ws%d" % first, align_bytes=64)
             for e in range(first, end):
                 lo, hi = (e - first) * PASSES * N, (e - first + 1) * PASSES * N
                 wq[e] = codes[:, lo:hi]
@@ -110,19 +117,29 @@ def tile_moe_shr_lin_bias_kernel(tc, x_words, x_scales, w, b, gate, offs, pos1, 
 
         late = S - GSLOTS
         gw = [keep.tile([P, S if o < PASSES - 1 else late], U32, name="gw%d" % o, align_bytes=64) for o in range(PASSES)]
-        gs = keep.tile([P, S], U8, name="gs", align_bytes=64)
+        gs = keep.tile([P, late], U8, name="gs", align_bytes=64)
+        grows = keep.tile([P, GSLOTS], U8, name="grows", align_bytes=64)
 
         def gather(dst, window, lo, hi):
             nc.vector.tensor_copy(dst, window.indirect(offs_sb[:, lo // 16 : hi // 16]))
 
         halves = ((0, S // 2), (S // 2, S))
+        gather(grows[:], rows[:], late, S)
+        for o in range(PASSES):
+            for j in range(4):
+                nc.sync.dma_start(
+                    out=late_scales[4 * o + j : P : 32, :].bitcast(I32),
+                    in_=grows[home[o] + j : home[o] + 16 : 4, :].bitcast(I32),
+                )
         for lo, hi in halves:
             gather(gw[0][:, lo:hi], xw[0][:].bitcast(U32), lo, hi)
-        for lo, hi in halves:
-            gather(gs[:, lo:hi], xs[:], lo, hi)
+        gather(gs[:], xs[:], 0, late)
         for lo, hi in halves:
             gather(gw[1][:, lo:hi], xw[1][:].bitcast(U32), lo, hi)
         quantize(*sets[0])
+        both_gates = keep.tile([P, 2 * T], F32, name="both_gates", tag="raw6", align_bytes=64)
+        nc.sync.dma_start(both_gates[:].rearrange("p (i t) -> p i t", i=2), gate.rearrange("i p t -> p i t"))
+        gates = [both_gates[:, i * T : (i + 1) * T] for i in range(2)]
         for lo in range(0, late, GSLOTS):
             gather(gw[2][:, lo : lo + GSLOTS], xw[2][:].bitcast(U32), lo, lo + GSLOTS)
         quantize(*sets[1])
@@ -139,7 +156,7 @@ def tile_moe_shr_lin_bias_kernel(tc, x_words, x_scales, w, b, gate, offs, pos1, 
                 lhsT=wq[e][:, o * N : (o + 1) * N].bitcast(FP8X4),
                 lhsT_scale=ws[e][:, o * N : (o + 1) * N],
                 rhs=words.bitcast(FP8X4),
-                rhs_scale=gs[4 * o : P, lo:hi],
+                rhs_scale=late_scales[4 * o : P, lo - late : hi - late] if lo >= late else gs[4 * o : P, lo:hi],
                 start=start,
                 stop=stop,
             )
@@ -192,7 +209,7 @@ def tile_moe_shr_lin_bias_kernel(tc, x_words, x_scales, w, b, gate, offs, pos1, 
         picks = []
 
         def pick(i, lo, hi):
-            picked = keep.tile([P, hi - lo], F32, name="pick%d_%d" % (i, lo), tag="raw%d" % (1 + len(picks)), align_bytes=64)
+            picked = keep.tile([P, hi - lo], F32, name="pick%d_%d" % (i, lo), tag="raw%d" % (1, 2, 3, 4, 5, 8, 9)[len(picks)], align_bytes=64)
             picks.append(picked)
             nc.vector.tensor_tensor(
                 picked[:], y[:].indirect(pos_sb[i][:, lo // 16 : hi // 16]), gates[i][:, lo:hi], MULT

@@ -39,8 +39,9 @@ def tile_moe_shr_lin_bias_kernel(tc, x_words, x_scales, w, b, gate, offs, pos1, 
 
         offs_sb = keep.tile([P, S // 16], U16, name="offs_sb")
         pos_sb = [keep.tile([P, T // 16], U16, name="pos%d" % i) for i in range(2)]
-        xw = [keep.tile([P, WINDOW if o < PASSES - 1 else T], I32, name="xw%d" % o, align_bytes=64) for o in range(PASSES)]
-        xs = keep.tile([P, 2 * WINDOW], U8, name="xs", align_bytes=64)
+        all_words = keep.tile([P, (PASSES - 1) * T + WINDOW], I32, name="all_words", align_bytes=64)
+        xw = [all_words[:, (PASSES - 1 - o) * T : (PASSES - 1 - o) * T + WINDOW] for o in range(PASSES)]
+        xs = keep.tile([P, T], U8, name="xs", align_bytes=64)
         rows = keep.tile([P, T], U8, name="rows", align_bytes=64)
         late_scales = keep.tile([P, GSLOTS], U8, name="late_scales", align_bytes=64)
         home = (0, 16, 80)
@@ -62,14 +63,12 @@ def tile_moe_shr_lin_bias_kernel(tc, x_words, x_scales, w, b, gate, offs, pos1, 
                 )
 
         all_rows = x_scales.rearrange("o f t -> (o f) t").bitcast(I32)
-        nc.vector.memset(xs[:, 0:T].bitcast(I32), 0)
-        nc.vector.memset(xs[:, T:].bitcast(I32), 0)
         nc.gpsimd.memset(rows[32:64, :].bitcast(I32), 0)
-        nc.gpsimd.memset(rows[96:P, :].bitcast(I32), 0)
-        for o in range(PASSES - 1):
-            nc.gpsimd.memset(xw[o][:, T:WINDOW], 0)
-        nc.gpsimd.memset(late_scales[:].bitcast(I32), 0)
         make_identity(nc, ident[:])
+        nc.vector.memset(xs[:].bitcast(I32), 0)
+        nc.vector.memset(rows[96:P, :].bitcast(I32), 0)
+        nc.vector.memset(xw[0][:, T:WINDOW], 0)
+        nc.vector.memset(late_scales[:].bitcast(I32), 0)
         nc.sync.dma_start(offs_sb[:], offs)
         nc.sync.dma_start(out=rows[0:32, :].bitcast(I32), in_=all_rows[0:32])
         nc.sync.dma_start(out=rows[64:96, :].bitcast(I32), in_=all_rows[16:48])
@@ -78,12 +77,12 @@ def tile_moe_shr_lin_bias_kernel(tc, x_words, x_scales, w, b, gate, offs, pos1, 
         load_w(1)
         load_scales()
         nc.sync.dma_start(bias[:], b)
-        for e in range(2, 6):
+        for e in range(2, 5):
             load_w(e)
         load_x(1)
         nc.sync.dma_start(pos_sb[0][:], pos1)
         nc.sync.dma_start(pos_sb[1][:], pos2)
-        for e in range(6, 10):
+        for e in range(5, 10):
             load_w(e)
         load_x(2)
         for e in range(10, E + 1):
@@ -132,20 +131,21 @@ def tile_moe_shr_lin_bias_kernel(tc, x_words, x_scales, w, b, gate, offs, pos1, 
                     in_=grows[home[o] + j : home[o] + 16 : 4, :].bitcast(I32),
                 )
         for lo, hi in halves:
-            gather(gw[0][:, lo:hi], xw[0][:].bitcast(U32), lo, hi)
-        gather(gs[:], xs[:], 0, late)
+            gather(gw[0][:, lo:hi], xw[0].bitcast(U32), lo, hi)
+        for lo in range(0, late, GSLOTS):
+            gather(gs[:, lo : lo + GSLOTS], xs[:], lo, lo + GSLOTS)
         for lo, hi in halves:
-            gather(gw[1][:, lo:hi], xw[1][:].bitcast(U32), lo, hi)
+            gather(gw[1][:, lo:hi], xw[1].bitcast(U32), lo, hi)
         quantize(*sets[0])
         both_gates = keep.tile([P, 2 * T], F32, name="both_gates", tag="raw6", align_bytes=64)
         nc.sync.dma_start(both_gates[:].rearrange("p (i t) -> p i t", i=2), gate.rearrange("i p t -> p i t"))
         gates = [both_gates[:, i * T : (i + 1) * T] for i in range(2)]
         for lo in range(0, late, GSLOTS):
-            gather(gw[2][:, lo : lo + GSLOTS], xw[2][:].bitcast(U32), lo, lo + GSLOTS)
+            gather(gw[2][:, lo : lo + GSLOTS], xw[2][:, 0:T].bitcast(U32), lo, lo + GSLOTS)
         quantize(*sets[1])
         last = keep.tile([P, GSLOTS], U32, name="last", tag="raw%d" % (E - 1), align_bytes=64)
         for lo, hi in ((0, 2 * C), (2 * C, 3 * C), (3 * C, 4 * C)):
-            gather(last[:, lo:hi], xw[2][:].bitcast(U32), late + lo, late + hi)
+            gather(last[:, lo:hi], xw[2][:, 0:T].bitcast(U32), late + lo, late + hi)
         quantize(*sets[2])
 
         def product(acc, o, lo, hi, start, stop):

@@ -31,6 +31,7 @@ def tile_moe_shr_lin_bias_kernel(tc, x_words, x_scales, w, b, gate, offs, pos1, 
     nc = tc.nc
     with ExitStack() as ctx:
         keep = ctx.enter_context(tc.tile_pool(name="keep", bufs=1))
+        lap = ctx.enter_context(tc.tile_pool(name="lap", bufs=1))
         psum = ctx.enter_context(tc.psum_pool(name="psum", bufs=1))
 
         edges = (0, 512, 768, 1024, 1280, 1536)
@@ -42,12 +43,12 @@ def tile_moe_shr_lin_bias_kernel(tc, x_words, x_scales, w, b, gate, offs, pos1, 
         all_words = keep.tile([P, (PASSES - 1) * T + WINDOW], I32, name="all_words", align_bytes=64)
         xw = [all_words[:, (PASSES - 1 - o) * T : (PASSES - 1 - o) * T + WINDOW] for o in range(PASSES)]
         xs = keep.tile([P, T], U8, name="xs", align_bytes=64)
-        rows = keep.tile([P, T], U8, name="rows", align_bytes=64)
+        rows = lap.tile([P, T], U8, name="rows", offset=0, align_bytes=64)
         late_scales = keep.tile([P, GSLOTS], U8, name="late_scales", align_bytes=64)
         home = (0, 16, 80)
         bias = keep.tile([P, E + 1], F32, name="bias")
         ident = keep.tile([P, P], F32, name="ident")
-        raw = [keep.tile([P, PASSES, 4, N], F32, name="raw%d" % e, align_bytes=64) for e in range(E + 1)]
+        raw = [keep.tile([P, PASSES, 4, N], F32, name="raw%d" % e, align_bytes=64) for e in range(E)]
 
         def load_w(e):
             nc.sync.dma_start(out=raw[e][:], in_=w[e].rearrange("(o p r) n -> p o r n", o=PASSES, r=4))
@@ -85,7 +86,7 @@ def tile_moe_shr_lin_bias_kernel(tc, x_words, x_scales, w, b, gate, offs, pos1, 
         for e in range(5, 10):
             load_w(e)
         load_x(2)
-        for e in range(10, E + 1):
+        for e in range(10, E):
             load_w(e)
 
         wq = {}
@@ -124,12 +125,15 @@ def tile_moe_shr_lin_bias_kernel(tc, x_words, x_scales, w, b, gate, offs, pos1, 
 
         halves = ((0, S // 2), (S // 2, S))
         gather(grows[:], rows[:], late, S)
-        for o in range(PASSES):
-            for j in range(4):
-                nc.sync.dma_start(
-                    out=late_scales[4 * o + j : P : 32, :].bitcast(I32),
-                    in_=grows[home[o] + j : home[o] + 16 : 4, :].bitcast(I32),
-                )
+        for m in range(4 * PASSES):
+            if m == 5:
+                raw.append(lap.tile([P, PASSES, 4, N], F32, name="raw_shared", offset=0, align_bytes=64))
+                load_w(E)
+            o, j = divmod(m, 4)
+            nc.sync.dma_start(
+                out=late_scales[4 * o + j : P : 32, :].bitcast(I32),
+                in_=grows[home[o] + j : home[o] + 16 : 4, :].bitcast(I32),
+            )
         for lo, hi in halves:
             gather(gw[0][:, lo:hi], xw[0].bitcast(U32), lo, hi)
         for lo in range(0, late, GSLOTS):
@@ -180,7 +184,7 @@ def tile_moe_shr_lin_bias_kernel(tc, x_words, x_scales, w, b, gate, offs, pos1, 
             for o in range(PASSES):
                 product(ends[j][:], o, S - C + j * P, S - C + (j + 1) * P, o == 0, o == PASSES - 1)
 
-        y = keep.tile([P, S], F32, name="y", tag="raw%d" % E, align_bytes=64)
+        y = lap.tile([P, S], F32, name="y", offset=0, align_bytes=64)
         for e in range(E - 1):
             nc.scalar.activation(out=y[:, e * C : (e + 1) * C], in_=accs[e], func=IDENT, bias=bias[:, e : e + 1])
         nc.scalar.activation(out=y[:, S - C : S - P], in_=ends[0][:], func=IDENT, bias=bias[:, E - 1 : E])

@@ -43,12 +43,13 @@ def tile_moe_shr_lin_bias_kernel(tc, x_words, x_scales, w, b, gate, offs, pos1, 
         all_words = keep.tile([P, (PASSES - 1) * T + WINDOW], I32, name="all_words", align_bytes=64)
         xw = [all_words[:, (PASSES - 1 - o) * T : (PASSES - 1 - o) * T + WINDOW] for o in range(PASSES)]
         xs = keep.tile([P, T], U8, name="xs", align_bytes=64)
-        rows = lap.tile([P, T], U8, name="rows", offset=0, align_bytes=64)
+        rows = lap.tile([P, T], U8, name="rows", offset=4 * (S + GSLOTS), align_bytes=64)
         late_scales = keep.tile([P, GSLOTS], U8, name="late_scales", align_bytes=64)
         home = (0, 16, 80)
         bias = keep.tile([P, E + 1], F32, name="bias")
         ident = keep.tile([P, P], F32, name="ident")
-        raw = [keep.tile([P, PASSES, 4, N], F32, name="raw%d" % e, align_bytes=64) for e in range(E)]
+        raw = [keep.tile([P, PASSES, 4, N], F32, name="raw%d" % e, align_bytes=64) for e in range(E - 1)]
+        raw.append(lap.tile([P, PASSES, 4, N], F32, name="raw_last", offset=4 * (S + GSLOTS - T), align_bytes=64))
 
         def load_w(e):
             nc.sync.dma_start(out=raw[e][:], in_=w[e].rearrange("(o p r) n -> p o r n", o=PASSES, r=4))
@@ -101,10 +102,13 @@ def tile_moe_shr_lin_bias_kernel(tc, x_words, x_scales, w, b, gate, offs, pos1, 
                 lo, hi = (e - first) * PASSES * N, (e - first + 1) * PASSES * N
                 wq[e] = codes[:, lo:hi]
                 ws[e] = scales[:, lo:hi]
-                nc.scalar.copy(
-                    out=stage[:, 4 * lo : 4 * hi].rearrange("p (o c i r) -> p o c r i", o=PASSES, i=2, r=4),
-                    in_=raw[e][:].rearrange("p o r (c i) -> p o c r i", i=2),
-                )
+                rounded = stage[:, 4 * lo : 4 * hi].rearrange("p (o c i r) -> p o c r i", o=PASSES, i=2, r=4)
+                loaded = raw[e][:].rearrange("p o r (c i) -> p o c r i", i=2)
+                if e < E:
+                    nc.scalar.copy(out=rounded, in_=loaded)
+                else:
+                    for o in range(PASSES):
+                        nc.gpsimd.tensor_scalar(rounded[:, o], loaded[:, o], 1.0, 0.0, MULT, ADD)
             lo = 0
             for width in (1024, 512, 256, 128):
                 while words - lo >= width:
@@ -127,7 +131,7 @@ def tile_moe_shr_lin_bias_kernel(tc, x_words, x_scales, w, b, gate, offs, pos1, 
         gather(grows[:], rows[:], late, S)
         for m in range(4 * PASSES):
             if m == 5:
-                raw.append(lap.tile([P, PASSES, 4, N], F32, name="raw_shared", offset=0, align_bytes=64))
+                raw.append(lap.tile([P, PASSES, 4, N], F32, name="raw_shared", offset=4 * (S + GSLOTS), align_bytes=64))
                 load_w(E)
             o, j = divmod(m, 4)
             nc.sync.dma_start(
@@ -147,7 +151,7 @@ def tile_moe_shr_lin_bias_kernel(tc, x_words, x_scales, w, b, gate, offs, pos1, 
         for lo in range(0, late, GSLOTS):
             gather(gw[2][:, lo : lo + GSLOTS], xw[2][:, 0:T].bitcast(U32), lo, lo + GSLOTS)
         quantize(*sets[1])
-        last = keep.tile([P, GSLOTS], U32, name="last", tag="raw%d" % (E - 1), align_bytes=64)
+        last = lap.tile([P, GSLOTS], U32, name="last", offset=4 * S, align_bytes=64)
         for lo, hi in ((0, 2 * C), (2 * C, 3 * C), (3 * C, 4 * C)):
             gather(last[:, lo:hi], xw[2][:, 0:T].bitcast(U32), late + lo, late + hi)
         quantize(*sets[2])

@@ -36,7 +36,6 @@ def tile_moe_shr_lin_bias_kernel(tc, x_words, x_scales, w, b, gate, offs, pos1, 
 
         edges = (0, 512, 768, 1024, 1280, 1536)
         chunks = list(zip(edges[:-1], edges[1:]))
-        sets = ((0, 8), (8, 12), (12, 13))
 
         offs_sb = keep.tile([P, S // 16], U16, name="offs_sb")
         pos_sb = [keep.tile([P, T // 16], U16, name="pos%d" % i) for i in range(2)]
@@ -90,34 +89,25 @@ def tile_moe_shr_lin_bias_kernel(tc, x_words, x_scales, w, b, gate, offs, pos1, 
         for e in range(10, E):
             load_w(e)
 
-        wq = {}
-        ws = {}
+        words = PASSES * N
+        stage = keep.tile([P, 4 * E * words], BF16, name="stage", align_bytes=64)
+        codes = keep.tile([P, E * words], U32, name="codes", align_bytes=64)
+        scales = keep.tile([P, E * words], U8, name="scales", align_bytes=64)
+        wq = [codes[:, e * words : (e + 1) * words] for e in range(E)]
+        ws = [scales[:, e * words : (e + 1) * words] for e in range(E)]
 
-        def quantize(first, end):
-            words = (end - first) * PASSES * N
-            stage = keep.tile([P, 4 * words], BF16, name="stage%d" % first, align_bytes=64)
-            codes = keep.tile([P, words], U32, name="wq%d" % first, align_bytes=64)
-            scales = keep.tile([P, words], U8, name="ws%d" % first, tag="grows" if first == E else "ws%d" % first, align_bytes=64)
-            for e in range(first, end):
-                lo, hi = (e - first) * PASSES * N, (e - first + 1) * PASSES * N
-                wq[e] = codes[:, lo:hi]
-                ws[e] = scales[:, lo:hi]
-                rounded = stage[:, 4 * lo : 4 * hi].rearrange("p (o c i r) -> p o c r i", o=PASSES, i=2, r=4)
-                loaded = raw[e][:].rearrange("p o r (c i) -> p o c r i", i=2)
-                if e < E:
-                    nc.scalar.copy(out=rounded, in_=loaded)
-                else:
-                    for o in range(PASSES):
-                        nc.gpsimd.tensor_scalar(rounded[:, o], loaded[:, o], 1.0, 0.0, MULT, ADD)
-            lo = 0
-            for width in (1024, 512, 256, 128):
-                while words - lo >= width:
-                    nc.vector.quantize_mx(
-                        out=codes[:, lo : lo + width].bitcast(FP8X4),
-                        scales=scales[:, lo : lo + width],
-                        in_=stage[:, 4 * lo : 4 * (lo + width)],
-                    )
-                    lo = lo + width
+        def interleaved(rounded, e):
+            return (
+                rounded.rearrange("p (o c i r) -> p o c r i", o=PASSES, i=2, r=4),
+                raw[e][:].rearrange("p o r (c i) -> p o c r i", i=2),
+            )
+
+        def round_w(e):
+            rounded, loaded = interleaved(stage[:, 4 * e * words : 4 * (e + 1) * words], e)
+            nc.scalar.copy(out=rounded, in_=loaded)
+
+        def quantize(into_codes, into_scales, rounded, lo, hi):
+            nc.vector.quantize_mx(out=into_codes[:, lo:hi].bitcast(FP8X4), scales=into_scales[:, lo:hi], in_=rounded[:, 4 * lo : 4 * hi])
 
         late = S - GSLOTS
         gw = [keep.tile([P, S if o < PASSES - 1 else late], U32, name="gw%d" % o, align_bytes=64) for o in range(PASSES)]
@@ -144,17 +134,29 @@ def tile_moe_shr_lin_bias_kernel(tc, x_words, x_scales, w, b, gate, offs, pos1, 
             gather(gs[:, lo : lo + GSLOTS], xs[:], lo, lo + GSLOTS)
         for lo, hi in halves:
             gather(gw[1][:, lo:hi], xw[1].bitcast(U32), lo, hi)
-        quantize(*sets[0])
+        for e in range(E):
+            round_w(e)
+        for lo, hi in ((0, 1024), (1024, 2048), (2048, 3072), (3072, 3584)):
+            quantize(codes, scales, stage, lo, hi)
         both_gates = keep.tile([P, 2 * T], F32, name="both_gates", tag="raw6", align_bytes=64)
         nc.sync.dma_start(both_gates[:].rearrange("p (i t) -> p i t", i=2), gate.rearrange("i p t -> p i t"))
         gates = [both_gates[:, i * T : (i + 1) * T] for i in range(2)]
         for lo in range(0, late, GSLOTS):
             gather(gw[2][:, lo : lo + GSLOTS], xw[2][:, 0:T].bitcast(U32), lo, lo + GSLOTS)
-        quantize(*sets[1])
+        quantize(codes, scales, stage, 3584, 4608)
         last = lap.tile([P, GSLOTS], U32, name="last", offset=4 * S, align_bytes=64)
         for lo, hi in ((0, 2 * C), (2 * C, 3 * C), (3 * C, 4 * C)):
             gather(last[:, lo:hi], xw[2][:, 0:T].bitcast(U32), late + lo, late + hi)
-        quantize(*sets[2])
+        shared_stage = keep.tile([P, 4 * words], BF16, name="shared_stage", align_bytes=64)
+        shared_codes = keep.tile([P, words], U32, name="shared_codes", align_bytes=64)
+        shared_scales = keep.tile([P, words], U8, name="shared_scales", tag="grows", align_bytes=64)
+        rounded, loaded = interleaved(shared_stage[:], E)
+        for o in range(PASSES):
+            nc.gpsimd.tensor_scalar(rounded[:, o], loaded[:, o], 1.0, 0.0, MULT, ADD)
+        for lo, hi in ((0, 2 * N), (2 * N, 3 * N)):
+            quantize(shared_codes, shared_scales, shared_stage, lo, hi)
+        wq.append(shared_codes)
+        ws.append(shared_scales)
 
         def product(acc, o, lo, hi, start, stop):
             e = lo // C
@@ -184,8 +186,7 @@ def tile_moe_shr_lin_bias_kernel(tc, x_words, x_scales, w, b, gate, offs, pos1, 
                 product(accs[e], o, e * C, (e + 1) * C, o == 0 and e == E - GROUP, o == PASSES - 1 and e > E - GROUP)
         for o in range(PASSES):
             product(accs[E - 2], o, S - 2 * C, S - C, o == 0, o == PASSES - 1)
-        for j in range(2):
-            for o in range(PASSES):
+            for j in range(2):
                 product(ends[j][:], o, S - C + j * P, S - C + (j + 1) * P, o == 0, o == PASSES - 1)
 
         y = lap.tile([P, S], F32, name="y", offset=0, align_bytes=64)

@@ -138,9 +138,17 @@ def tile_moe_shr_lin_bias_kernel(tc, x_words, x_scales, w, b, gate, offs, pos1, 
             round_w(e)
         for lo, hi in ((0, 1024), (1024, 2048), (2048, 3072), (3072, 3584)):
             quantize(codes, scales, stage, lo, hi)
-        both_gates = keep.tile([P, 2 * T], F32, name="both_gates", tag="raw6", align_bytes=64)
-        nc.sync.dma_start(both_gates[:].rearrange("p (i t) -> p i t", i=2), gate.rearrange("i p t -> p i t"))
-        gates = [both_gates[:, i * T : (i + 1) * T] for i in range(2)]
+        gate_parts = []
+        for part, (lo, hi) in enumerate(((0, BANK), (BANK, T))):
+            both = keep.tile([P, 2 * (hi - lo)], F32, name="gates%d" % part, tag="raw%d" % (6 + part), align_bytes=64)
+            nc.sync.dma_start(both[:].rearrange("p (i t) -> p i t", i=2), gate[:, :, lo:hi].rearrange("i p t -> p i t"))
+            gate_parts.append(both)
+
+        def gates(i, lo, hi):
+            if lo < BANK:
+                return gate_parts[0][:, i * BANK + lo : i * BANK + hi]
+            return gate_parts[1][:, i * (T - BANK) + lo - BANK : i * (T - BANK) + hi - BANK]
+
         for lo in range(0, late, GSLOTS):
             gather(gw[2][:, lo : lo + GSLOTS], xw[2][:, 0:T].bitcast(U32), lo, lo + GSLOTS)
         quantize(codes, scales, stage, 3584, 4608)
@@ -221,7 +229,7 @@ def tile_moe_shr_lin_bias_kernel(tc, x_words, x_scales, w, b, gate, offs, pos1, 
             picked = keep.tile([P, hi - lo], F32, name="pick%d_%d" % (i, lo), tag="raw%d" % (1, 2, 3, 4, 5, 8, 9)[len(picks)], align_bytes=64)
             picks.append(picked)
             nc.vector.tensor_tensor(
-                picked[:], y[:].indirect(pos_sb[i][:, lo // 16 : hi // 16]), gates[i][:, lo:hi], MULT
+                picked[:], y[:].indirect(pos_sb[i][:, lo // 16 : hi // 16]), gates(i, lo, hi), MULT
             )
             return picked
 

@@ -17,14 +17,18 @@ FP8X4 = mybir.dt.float8_e4m3fn_x4
 MULT = mybir.AluOpType.mult
 ADD = mybir.AluOpType.add
 IDENT = mybir.ActivationFunctionType.Identity
+COPY = mybir.ActivationFunctionType.Copy
 
 P = 128
 PASSES = 3
-GROUP = 4
-GROUPS = E // GROUP
-GSLOTS = GROUP * C
 BANK = 512
 WINDOW = 2048
+LATE = 4 * C
+EARLY = S - LATE
+WORDS = PASSES * N
+RAW = 4 * 4 * WORDS
+TURNED = 11
+UNIT = 256
 
 
 def tile_moe_shr_lin_bias_kernel(tc, x_words, x_scales, w, b, gate, offs, pos1, pos2, out):
@@ -34,259 +38,265 @@ def tile_moe_shr_lin_bias_kernel(tc, x_words, x_scales, w, b, gate, offs, pos1, 
         lap = ctx.enter_context(tc.tile_pool(name="lap", bufs=1))
         psum = ctx.enter_context(tc.psum_pool(name="psum", bufs=1))
 
-        edges = (0, 512, 768, 1024, 1280, 1536)
-        chunks = list(zip(edges[:-1], edges[1:]))
-
         offs_sb = keep.tile([P, S // 16], U16, name="offs_sb")
         pos_sb = [keep.tile([P, T // 16], U16, name="pos%d" % i) for i in range(2)]
         all_words = keep.tile([P, (PASSES - 1) * T + WINDOW], I32, name="all_words", align_bytes=64)
-        xw = [all_words[:, (PASSES - 1 - o) * T : (PASSES - 1 - o) * T + WINDOW] for o in range(PASSES)]
+        first_col = [(PASSES - 1 - o) * T for o in range(PASSES)]
         xs = keep.tile([P, T], U8, name="xs", align_bytes=64)
-        rows = lap.tile([P, T], U8, name="rows", offset=4 * (S + GSLOTS), align_bytes=64)
-        late_scales = keep.tile([P, GSLOTS], U8, name="late_scales", align_bytes=64)
-        home = (0, 16, 80)
+        rows = keep.tile([P, T], U8, name="rows", align_bytes=64)
+        late_scales = keep.tile([P, LATE], U8, name="late_scales", align_bytes=64)
         bias = keep.tile([P, E + 1], F32, name="bias")
         ident = keep.tile([P, P], F32, name="ident")
-        raw = [keep.tile([P, PASSES, 4, N], F32, name="raw%d" % e, align_bytes=64) for e in range(E - 1)]
-        raw.append(lap.tile([P, PASSES, 4, N], F32, name="raw_last", offset=4 * (S + GSLOTS - T), align_bytes=64))
+        gate_rows = keep.tile([P, P], F32, name="gate_rows")
+        gate_cols = keep.tile([P, TURNED], F32, name="gate_cols")
+
+        order = [E] + list(range(E))
+        raw = {e: keep.tile([P, PASSES, 4, N], F32, name="raw%d" % e, align_bytes=64) for e in order[:-3]}
+        last_raw = 4 * S - 2048
+        raw[E - 1] = lap.tile([P, PASSES, 4, N], F32, name="raw_last", offset=last_raw, align_bytes=64)
+        raw[E - 2] = lap.tile([P, PASSES, 4, N], F32, name="raw_before_last", offset=last_raw + RAW, align_bytes=64)
+        third_raw = last_raw + 2 * RAW
+        raw[E - 3] = lap.tile([P, PASSES, 4, N], F32, name="raw_third_last", offset=third_raw, align_bytes=64)
+
+        def xw(o, lo, hi):
+            return all_words[:, first_col[o] + lo : first_col[o] + hi]
 
         def load_w(e):
             nc.sync.dma_start(out=raw[e][:], in_=w[e].rearrange("(o p r) n -> p o r n", o=PASSES, r=4))
 
         def load_x(o):
-            nc.sync.dma_start(out=xw[o][:, 0:T], in_=x_words[o].rearrange("p t r -> p (t r)").bitcast(I32))
+            nc.sync.dma_start(out=xw(o, 0, T), in_=x_words[o].rearrange("p t r -> p (t r)").bitcast(I32))
 
-        def load_scales():
-            for q in range(4):
-                nc.sync.dma_start(
-                    out=xs[32 * q : 32 * q + 4 * PASSES, 0:T].bitcast(I32),
-                    in_=x_scales[:, 4 * q : 4 * q + 4, :].bitcast(I32),
-                )
-
+        row0 = 48
         all_rows = x_scales.rearrange("o f t -> (o f) t").bitcast(I32)
-        nc.gpsimd.memset(rows[32:64, :].bitcast(I32), 0)
+        nc.gpsimd.memset(rows[0:row0, :].bitcast(I32), 0)
         make_identity(nc, ident[:])
-        nc.vector.memset(xs[:].bitcast(I32), 0)
+        nc.gpsimd.memset(gate_rows[:], 0.0)
         nc.vector.memset(rows[96:P, :].bitcast(I32), 0)
-        nc.vector.memset(xw[0][:, T:WINDOW], 0)
+        nc.vector.memset(xs[:].bitcast(I32), 0)
+        nc.vector.memset(xw(0, T, WINDOW), 0)
         nc.vector.memset(late_scales[:].bitcast(I32), 0)
+
         nc.sync.dma_start(offs_sb[:], offs)
-        nc.sync.dma_start(out=rows[0:32, :].bitcast(I32), in_=all_rows[0:32])
         nc.sync.dma_start(out=rows[64:96, :].bitcast(I32), in_=all_rows[16:48])
+        nc.sync.dma_start(out=rows[row0:64, :].bitcast(I32), in_=all_rows[0:16])
         load_x(0)
-        load_w(0)
-        load_w(1)
-        load_scales()
+        load_w(order[0])
+        load_w(order[1])
+        for q in range(4):
+            nc.sync.dma_start(
+                out=xs[32 * q : 32 * q + 4 * PASSES, :].bitcast(I32),
+                in_=x_scales[:, 4 * q : 4 * q + 4, :].bitcast(I32),
+            )
+        nc.sync.dma_start(out=gate_rows[0:TURNED, :], in_=gate[1, 0, 0 : TURNED * P].rearrange("(c t) -> c t", t=P))
         nc.sync.dma_start(bias[:], b)
-        for e in range(2, 5):
+        for e in order[2:5]:
             load_w(e)
         load_x(1)
         nc.sync.dma_start(pos_sb[0][:], pos1)
         nc.sync.dma_start(pos_sb[1][:], pos2)
-        for e in range(5, 10):
+        for e in order[5:10]:
             load_w(e)
         load_x(2)
-        for e in range(10, E):
+        for e in order[10:]:
             load_w(e)
 
-        words = PASSES * N
-        stage = keep.tile([P, 4 * E * words], BF16, name="stage", align_bytes=64)
-        codes = keep.tile([P, E * words], U32, name="codes", align_bytes=64)
-        scales = keep.tile([P, E * words], U8, name="scales", align_bytes=64)
-        wq = [codes[:, e * words : (e + 1) * words] for e in range(E)]
-        ws = [scales[:, e * words : (e + 1) * words] for e in range(E)]
+        stage = keep.tile([P, 4 * (E + 1) * WORDS], BF16, name="stage", align_bytes=64)
+        codes = keep.tile([P, (E + 1) * WORDS], U32, name="codes", align_bytes=64)
+        scales = keep.tile([P, (E + 1) * WORDS], U8, name="scales", align_bytes=64)
 
-        def interleaved(rounded, e):
+        def matrix(tile, e, o):
+            at = order.index(e) * WORDS + o * N
+            return tile[:, at : at + N]
+
+        def interleaved(e):
+            at = 4 * order.index(e) * WORDS
             return (
-                rounded.rearrange("p (o c i r) -> p o c r i", o=PASSES, i=2, r=4),
+                stage[:, at : at + 4 * WORDS].rearrange("p (o c i r) -> p o c r i", o=PASSES, i=2, r=4),
                 raw[e][:].rearrange("p o r (c i) -> p o c r i", i=2),
             )
 
-        def round_w(e):
-            rounded, loaded = interleaved(stage[:, 4 * e * words : 4 * (e + 1) * words], e)
-            nc.scalar.copy(out=rounded, in_=loaded)
-
-        def quantize(into_codes, into_scales, rounded, lo, hi):
-            nc.vector.quantize_mx(out=into_codes[:, lo:hi].bitcast(FP8X4), scales=into_scales[:, lo:hi], in_=rounded[:, 4 * lo : 4 * hi])
-
-        late = S - GSLOTS
-        gw = [keep.tile([P, S if o < PASSES - 1 else late], U32, name="gw%d" % o, align_bytes=64) for o in range(PASSES)]
-        gs = keep.tile([P, late], U8, name="gs", align_bytes=64)
-        grows = keep.tile([P, GSLOTS], U8, name="grows", align_bytes=64)
+        def quantize(lo, hi):
+            nc.vector.quantize_mx(out=codes[:, lo:hi].bitcast(FP8X4), scales=scales[:, lo:hi], in_=stage[:, 4 * lo : 4 * hi])
 
         def gather(dst, window, lo, hi):
             nc.vector.tensor_copy(dst, window.indirect(offs_sb[:, lo // 16 : hi // 16]))
 
-        halves = ((0, S // 2), (S // 2, S))
-        gather(grows[:], rows[:], late, S)
-        for m in range(4 * PASSES):
-            if m == 5:
-                raw.append(lap.tile([P, PASSES, 4, N], F32, name="raw_shared", offset=4 * (S + GSLOTS), align_bytes=64))
-                load_w(E)
-            o, j = divmod(m, 4)
-            nc.sync.dma_start(
-                out=late_scales[4 * o + j : P : 32, :].bitcast(I32),
-                in_=grows[home[o] + j : home[o] + 16 : 4, :].bitcast(I32),
-            )
-        for lo, hi in halves:
-            gather(gw[0][:, lo:hi], xw[0].bitcast(U32), lo, hi)
-        for lo in range(0, late, GSLOTS):
-            gather(gs[:, lo : lo + GSLOTS], xs[:], lo, lo + GSLOTS)
-        for lo, hi in halves:
-            gather(gw[1][:, lo:hi], xw[1].bitcast(U32), lo, hi)
-        for e in range(E):
-            round_w(e)
-        for lo, hi in ((0, 1024), (1024, 2048), (2048, 3072), (3072, 3584)):
-            quantize(codes, scales, stage, lo, hi)
-        gate_parts = []
-        for part, (lo, hi) in enumerate(((0, BANK), (BANK, T))):
-            both = keep.tile([P, 2 * (hi - lo)], F32, name="gates%d" % part, tag="raw%d" % (6 + part), align_bytes=64)
-            nc.sync.dma_start(both[:].rearrange("p (i t) -> p i t", i=2), gate[:, :, lo:hi].rearrange("i p t -> p i t"))
-            gate_parts.append(both)
+        grows = keep.tile([P, LATE], U8, name="grows", align_bytes=64)
+        gs = keep.tile([P, EARLY], U8, name="gs", align_bytes=64)
+        gw = [keep.tile([P, S if o < PASSES - 1 else EARLY], U32, name="gw%d" % o, align_bytes=64) for o in range(PASSES)]
 
-        def gates(i, lo, hi):
-            if lo < BANK:
-                return gate_parts[0][:, i * BANK + lo : i * BANK + hi]
-            return gate_parts[1][:, i * (T - BANK) + lo - BANK : i * (T - BANK) + hi - BANK]
-
-        for lo in range(0, late, GSLOTS):
-            gather(gw[2][:, lo : lo + GSLOTS], xw[2][:, 0:T].bitcast(U32), lo, lo + GSLOTS)
-        quantize(codes, scales, stage, 3584, 4608)
-        last = lap.tile([P, GSLOTS], U32, name="last", offset=4 * S, align_bytes=64)
-        for lo, hi in ((0, 2 * C), (2 * C, 3 * C), (3 * C, 4 * C)):
-            gather(last[:, lo:hi], xw[2][:, 0:T].bitcast(U32), late + lo, late + hi)
-        shared_stage = keep.tile([P, 4 * words], BF16, name="shared_stage", align_bytes=64)
-        shared_codes = keep.tile([P, words], U32, name="shared_codes", align_bytes=64)
-        shared_scales = keep.tile([P, words], U8, name="shared_scales", tag="grows", align_bytes=64)
-        rounded, loaded = interleaved(shared_stage[:], E)
+        gather(grows[:], rows[:], EARLY, S)
         for o in range(PASSES):
-            nc.gpsimd.tensor_scalar(rounded[:, o], loaded[:, o], 1.0, 0.0, MULT, ADD)
-        for lo, hi in ((0, 2 * N), (2 * N, 3 * N)):
-            quantize(shared_codes, shared_scales, shared_stage, lo, hi)
-        wq.append(shared_codes)
-        ws.append(shared_scales)
+            for j in range(4):
+                nc.sync.dma_start(
+                    out=late_scales[4 * o + j : P : 32, :].bitcast(I32),
+                    in_=grows[row0 + 16 * o + j : row0 + 16 * o + 16 : 4, :].bitcast(I32),
+                )
+        rest = T - TURNED * P
+        gates = keep.tile([P, T], F32, name="gates", tag="raw0", align_bytes=64)
+        rest_gates = keep.tile([P, rest], F32, name="rest_gates", align_bytes=64)
+        nc.sync.dma_start(rest_gates[:], gate[1, :, TURNED * P : T])
+        nc.sync.dma_start(gates[:], gate[0])
+
+        halves = ((0, S // 2), (S // 2, S))
+        for lo, hi in halves:
+            gather(gw[0][:, lo:hi], xw(0, 0, WINDOW).bitcast(U32), lo, hi)
+        for lo in range(0, EARLY, LATE):
+            gather(gs[:, lo : lo + LATE], xs[:], lo, lo + LATE)
+        for e in order:
+            rounded, loaded = interleaved(e)
+            if e == E - 2:
+                for o in range(PASSES):
+                    nc.gpsimd.tensor_scalar(rounded[:, o], loaded[:, o], 1.0, 0.0, MULT, ADD)
+            else:
+                nc.scalar.copy(out=rounded, in_=loaded)
+        quantize(0, 1024)
+        for lo, hi in halves:
+            gather(gw[1][:, lo:hi], xw(1, 0, WINDOW).bitcast(U32), lo, hi)
+        quantize(1024, 2048)
+        quantize(2048, 3072)
+        gather(gw[2][:], xw(2, 0, 2 * WINDOW).bitcast(U32), 0, EARLY)
+        quantize(3072, 4096)
+        next_words = lap.tile([P, 2 * C], U32, name="next_words", offset=third_raw, align_bytes=64)
+        gather(next_words[:], xw(2, 0, T).bitcast(U32), EARLY, EARLY + 2 * C)
+        quantize(4096, 4608)
+        quantize(4608, 4992)
+        last_words = lap.tile([P, 2 * C], U32, name="last_words", offset=last_raw + RAW - 4 * C, align_bytes=64)
+        for lo in (0, C):
+            gather(last_words[:, lo : lo + C], xw(2, 0, T).bitcast(U32), S - 2 * C + lo, S - C + lo)
+
+        turned_gates = psum.tile([P, P], F32, name="turned_gates", tag="bank7")
+        nc.tensor.transpose(turned_gates[:], gate_rows[:], ident[:])
+        nc.scalar.copy(out=gate_cols[:], in_=turned_gates[:, 0:TURNED])
+
+        shared_sums = [psum.tile([P, BANK], F32, name="shared%d" % c, tag="bank%d" % (4 + c)) for c in range(T // BANK)]
+        for o in range(PASSES):
+            for lo in range(0, T, P):
+                nc.tensor.matmul_mx(
+                    out=shared_sums[lo // BANK][:, lo % BANK : lo % BANK + P],
+                    lhsT=xw(o, lo, lo + P).bitcast(FP8X4),
+                    lhsT_scale=xs[4 * o : P, lo : lo + P],
+                    rhs=matrix(codes, E, o).bitcast(FP8X4),
+                    rhs_scale=matrix(scales, E, o),
+                    start=(o == 0 and lo % BANK == 0),
+                    stop=(o == PASSES - 1 and lo % BANK == BANK - P),
+                )
+        shared = keep.tile([P, T], F32, name="shared", tag="raw%d" % E, align_bytes=64)
+        for c in range(T // BANK):
+            nc.scalar.copy(out=shared[:, c * BANK : (c + 1) * BANK], in_=shared_sums[c][:])
+
+        edges = (0, 512, 768, 1024, 1280, 1536)
+        sum_banks = (0, 1, 2, 7, 3)
+        totals = {}
+
+        def open_total(c):
+            lo, hi = edges[c], edges[c + 1]
+            totals[c] = psum.tile([P, hi - lo], F32, name="total%d" % c, tag="bank%d" % sum_banks[c])
+            for at in range(lo, hi, P):
+                nc.tensor.matmul(
+                    totals[c][:, at - lo : at - lo + P], shared[:, at : at + P], ident[:],
+                    is_transpose=True, start=(at == lo), stop=False,
+                )
+
+        for c in range(3):
+            open_total(c)
 
         def product(acc, o, lo, hi, start, stop):
             e = lo // C
-            words = last[:, lo - late : hi - late] if (o == PASSES - 1 and lo >= late) else gw[o][:, lo:hi]
+            if o < PASSES - 1 or lo < EARLY:
+                words = gw[o][:, lo:hi]
+            elif lo < S - 2 * C:
+                words = next_words[:, lo - EARLY : hi - EARLY]
+            else:
+                words = last_words[:, lo - (S - 2 * C) : hi - (S - 2 * C)]
             nc.tensor.matmul_mx(
                 out=acc,
-                lhsT=wq[e][:, o * N : (o + 1) * N].bitcast(FP8X4),
-                lhsT_scale=ws[e][:, o * N : (o + 1) * N],
+                lhsT=matrix(codes, e, o).bitcast(FP8X4),
+                lhsT_scale=matrix(scales, e, o),
                 rhs=words.bitcast(FP8X4),
-                rhs_scale=late_scales[4 * o : P, lo - late : hi - late] if lo >= late else gs[4 * o : P, lo:hi],
+                rhs_scale=late_scales[4 * o : P, lo - EARLY : hi - EARLY] if lo >= EARLY else gs[4 * o : P, lo:hi],
                 start=start,
                 stop=stop,
             )
 
-        accs = []
-        for h in range(E // 2 - 1):
-            pair = psum.tile([P, 2, C], F32, name="pair%d" % h, tag="bank%d" % h)
-            accs.extend([pair[:, 0, :], pair[:, 1, :]])
-        lone = psum.tile([P, C], F32, name="lone", tag="bank%d" % (E // 2 - 1))
-        accs.append(lone[:])
-        ends = [psum.tile([P, P], F32, name="end%d" % j, tag="bank%d" % (E // 2 + j)) for j in range(2)]
-        for e in range(E - GROUP):
-            for o in range(PASSES):
-                product(accs[e], o, e * C, (e + 1) * C, o == 0, o == PASSES - 1)
-        for o in range(PASSES):
-            for e in (E - GROUP, E - GROUP + 1):
-                product(accs[e], o, e * C, (e + 1) * C, o == 0 and e == E - GROUP, o == PASSES - 1 and e > E - GROUP)
-        for o in range(PASSES):
-            product(accs[E - 2], o, S - 2 * C, S - C, o == 0, o == PASSES - 1)
-            for j in range(2):
-                product(ends[j][:], o, S - C + j * P, S - C + (j + 1) * P, o == 0, o == PASSES - 1)
-
         y = lap.tile([P, S], F32, name="y", offset=0, align_bytes=64)
-        for e in range(E - 1):
-            nc.scalar.activation(out=y[:, e * C : (e + 1) * C], in_=accs[e], func=IDENT, bias=bias[:, e : e + 1])
-        nc.scalar.activation(out=y[:, S - C : S - P], in_=ends[0][:], func=IDENT, bias=bias[:, E - 1 : E])
-        nc.scalar.activation(out=y[:, S - P : S], in_=ends[1][:], func=IDENT, bias=bias[:, E - 1 : E])
 
-        shared_banks = []
-        for c in range(T // BANK):
-            acc = psum.tile([P, BANK], F32, name="shared%d" % c, tag="bank%d" % c)
-            shared_banks.append(acc)
+        def empty(acc, lo, hi):
+            e = lo // C
+            nc.scalar.activation(out=y[:, lo:hi], in_=acc, func=IDENT, bias=bias[:, e : e + 1])
+
+        pairs = [psum.tile([P, 2, C], F32, name="pair%d" % h, tag="bank%d" % (3 + h)) for h in range(E // 2 - 1)]
+        for first, end in ((0, 4), (4, 5)):
             for o in range(PASSES):
-                nc.tensor.matmul_mx(
-                    out=acc[:],
-                    lhsT=wq[E][:, o * N : (o + 1) * N].bitcast(FP8X4),
-                    lhsT_scale=ws[E][:, o * N : (o + 1) * N],
-                    rhs=xw[o][:, c * BANK : (c + 1) * BANK].bitcast(FP8X4),
-                    rhs_scale=xs[4 * o : P, c * BANK : (c + 1) * BANK],
-                    start=(o == 0),
-                    stop=(o == PASSES - 1),
+                for e in range(2 * first, 2 * end):
+                    product(pairs[e // 2][:, e % 2, :], o, e * C, (e + 1) * C, o == 0 and e % 2 == 0, o == PASSES - 1 and e % 2 == 1)
+            for e in range(2 * first, 2 * end):
+                empty(pairs[e // 2][:, e % 2, :], e * C, (e + 1) * C)
+        ends = ((S - 2 * C, S - C), (S - C, S - P), (S - P, S))
+        lone = [psum.tile([P, hi - lo], F32, name="lone%d" % j, tag="bank%d" % (3 + j)) for j, (lo, hi) in enumerate(ends)]
+        for o in range(PASSES):
+            for j, (lo, hi) in enumerate(ends):
+                product(lone[j][:], o, lo, hi, o == 0, o == PASSES - 1)
+        for j, (lo, hi) in enumerate(ends):
+            empty(lone[j][:], lo, hi)
+        for c in (3, 4):
+            open_total(c)
+
+        units = [(lo, min(lo + UNIT, TURNED * P)) for lo in range(0, TURNED * P, UNIT)]
+        second = keep.tile([P, 2 * UNIT], F32, name="second", tag="raw1", align_bytes=64)
+        gated = keep.tile([P, TURNED * P], F32, name="gated", tag="raw2", align_bytes=64)
+        first = keep.tile([P, T - UNIT], F32, name="first", tag="raw3", align_bytes=64)
+        rest_second = keep.tile([P, rest], F32, name="rest_second", tag="raw4", align_bytes=64)
+        res = keep.tile([P, T], F32, name="res", tag="raw5", align_bytes=64)
+        forward = {}
+
+        def fetch_second(u):
+            lo, hi = units[u]
+            picked = second[:, (u % 2) * UNIT : (u % 2) * UNIT + hi - lo]
+            nc.scalar.activation(picked, y[:].indirect(pos_sb[1][:, lo // 16 : hi // 16]), COPY)
+            forward[u] = psum.tile([P, hi - lo], F32, name="forward%d" % u, tag="bank%d" % (6 - u % 3))
+            for at in range(0, hi - lo, P):
+                nc.tensor.transpose(forward[u][:, at : at + P], picked[:, at : at + P], ident[:])
+
+        def gate_second(u):
+            lo, hi = units[u]
+            for at in range(lo, hi, P):
+                nc.scalar.activation(
+                    out=gated[:, at : at + P], in_=forward[u][:, at - lo : at - lo + P], func=COPY,
+                    scale=gate_cols[:, at // P : at // P + 1],
                 )
-
-        shared = keep.tile([P, T], F32, name="shared", tag="raw0", align_bytes=64)
-        for c in range(T // BANK):
-            lo, hi = c * BANK, (c + 1) * BANK
-            nc.scalar.activation(out=shared[:, lo:hi], in_=shared_banks[c][:], func=IDENT, bias=bias[:, E : E + 1])
-
-        picks = []
-
-        def pick(i, lo, hi):
-            picked = keep.tile([P, hi - lo], F32, name="pick%d_%d" % (i, lo), tag="raw%d" % (1, 2, 3, 4, 5, 8, 9)[len(picks)], align_bytes=64)
-            picks.append(picked)
-            nc.vector.tensor_tensor(
-                picked[:], y[:].indirect(pos_sb[i][:, lo // 16 : hi // 16]), gates(i, lo, hi), MULT
-            )
-            return picked
-
-        sum_banks = (3, 4, 5, 6, 7)
-        back_banks = (0, 1, 2, 3, 4)
-        totals = [
-            psum.tile([P, hi - lo], F32, name="total%d" % c, tag="bank%d" % sum_banks[c])
-            for c, (lo, hi) in enumerate(chunks)
-        ]
-
-        def turn_onto(c, term, start, stop):
-            blocks = (chunks[c][1] - chunks[c][0]) // P
-            for k in range(blocks):
+            c = max(k for k in range(len(edges) - 1) if edges[k] <= lo)
+            for at in range(lo, hi, P):
                 nc.tensor.matmul(
-                    totals[c][:, k * P : (k + 1) * P], term[:, k * P : (k + 1) * P], ident[:], is_transpose=True,
-                    start=(start and k == 0), stop=(stop and k == blocks - 1),
+                    totals[c][:, at - edges[c] : at - edges[c] + P], gated[:, at : at + P], ident[:],
+                    is_transpose=True, start=False, stop=(at + P == min(edges[c + 1], TURNED * P)),
                 )
 
-        def empty(c):
-            turned = keep.tile([P, chunks[c][1] - chunks[c][0]], F32, name="turned%d" % c)
-            nc.scalar.copy(out=turned[:], in_=totals[c][:])
-            return turned
+        fetch_second(0)
+        for u in range(1, len(units)):
+            fetch_second(u)
+            gate_second(u - 1)
+        gate_second(len(units) - 1)
 
-        def turn_back(c, turned):
-            width = chunks[c][1] - chunks[c][0]
-            back = psum.tile([P, width], F32, name="back%d" % c, tag="bank%d" % back_banks[c])
-            for k in range(width // P):
-                nc.tensor.transpose(back[:, k * P : (k + 1) * P], turned[:, k * P : (k + 1) * P], ident[:])
-            return back
+        def firsts(lo, hi):
+            at = lo % (T - UNIT)
+            return first[:, at : at + hi - lo]
 
-        def store(c, back):
-            lo, hi = chunks[c]
-            res = keep.tile([P, hi - lo], F32, name="res%d" % c)
-            nc.scalar.copy(out=res[:], in_=back[:])
-            nc.sync.dma_start(out=out[:, lo:hi], in_=res[:])
+        def fetch_first(lo, hi):
+            nc.vector.tensor_tensor(firsts(lo, hi), y[:].indirect(pos_sb[0][:, lo // 16 : hi // 16]), gates[:, lo:hi], MULT)
 
-        lo, hi = chunks[0]
-        turn_onto(0, shared[:, lo:hi], True, False)
-        turn_onto(0, pick(0, lo, hi)[:], False, False)
-        turn_onto(0, pick(1, lo, hi)[:], False, True)
-        store(0, turn_back(0, empty(0)))
+        def finish(c):
+            lo, hi = edges[c], edges[c + 1]
+            nc.vector.scalar_tensor_tensor(res[:, lo:hi], totals[c][:], bias[:, E : E + 1], firsts(lo, hi), ADD, ADD)
+            nc.sync.dma_start(out=out[:, lo:hi], in_=res[:, lo:hi])
 
-        first_pick = pick(0, edges[1], edges[4])
-        for c in (1, 2, 3, 4):
-            turn_onto(c, shared[:, edges[c] : edges[c + 1]], True, False)
-        for c in (1, 2, 3):
-            turn_onto(c, first_pick[:, edges[c] - edges[1] : edges[c + 1] - edges[1]], False, c > 1)
-        turn_onto(1, pick(1, *chunks[1])[:], False, True)
-        turn_onto(4, pick(0, *chunks[4])[:], False, True)
-        turned = {c: empty(c) for c in (1, 2, 3, 4)}
-        backs = {c: turn_back(c, turned[c]) for c in (1, 2, 3, 4)}
-        store(1, backs[1])
-
-        wide = pick(1, edges[2], edges[4])
-        second_picks = {2: wide[:, 0:C], 3: wide[:, C : 2 * C], 4: pick(1, *chunks[4])[:]}
+        fetch_first(edges[0], edges[1])
+        fetch_first(edges[1], edges[4])
+        nc.vector.tensor_tensor(rest_second[:], y[:].indirect(pos_sb[1][:, TURNED * P // 16 : T // 16]), rest_gates[:], MULT)
+        finish(0)
+        fetch_first(edges[4], edges[5])
+        finish(1)
+        nc.vector.tensor_tensor(firsts(T - rest, T), firsts(T - rest, T), rest_second[:], ADD)
         for c in (2, 3, 4):
-            lo, hi = chunks[c]
-            res = keep.tile([P, hi - lo], F32, name="res%d" % c)
-            nc.vector.tensor_tensor(res[:], backs[c][:], second_picks[c], ADD)
-            nc.sync.dma_start(out=out[:, lo:hi], in_=res[:])
+            finish(c)

@@ -112,8 +112,8 @@ def tile_moe_shr_lin_bias_kernel(tc, x_words, x_scales, w, b, gate, offs, pos1, 
         def interleaved(e):
             at = 4 * order.index(e) * WORDS
             return (
-                stage[:, at : at + 4 * WORDS].rearrange("p (o c i r) -> p o c r i", o=PASSES, i=2, r=4),
-                raw[e][:].rearrange("p o r (c i) -> p o c r i", i=2),
+                stage[:, at : at + 4 * WORDS].rearrange("p (o c i r) -> p o c r i", o=PASSES, i=4, r=4),
+                raw[e][:].rearrange("p o r (c i) -> p o c r i", i=4),
             )
 
         def quantize(lo, hi):
@@ -146,11 +146,7 @@ def tile_moe_shr_lin_bias_kernel(tc, x_words, x_scales, w, b, gate, offs, pos1, 
             gather(gs[:, lo : lo + LATE], xs[:], lo, lo + LATE)
         for e in order:
             rounded, loaded = interleaved(e)
-            if e == E - 2:
-                for o in range(PASSES):
-                    nc.gpsimd.tensor_scalar(rounded[:, o], loaded[:, o], 1.0, 0.0, MULT, ADD)
-            else:
-                nc.scalar.copy(out=rounded, in_=loaded)
+            nc.scalar.copy(out=rounded, in_=loaded)
         quantize(0, 1024)
         for lo, hi in halves:
             gather(gw[1][:, lo:hi], xw(1, 0, WINDOW).bitcast(U32), lo, hi)

@@ -29,6 +29,7 @@ WORDS = PASSES * N
 RAW = 4 * 4 * WORDS
 TURNED = 11
 UNIT = 256
+AHEAD = 2
 
 
 def tile_moe_shr_lin_bias_kernel(tc, x_words, x_scales, w, b, gate, offs, pos1, pos2, out):
@@ -42,7 +43,7 @@ def tile_moe_shr_lin_bias_kernel(tc, x_words, x_scales, w, b, gate, offs, pos1, 
         pos_sb = [keep.tile([P, T // 16], U16, name="pos%d" % i) for i in range(2)]
         all_words = keep.tile([P, (PASSES - 1) * T + WINDOW], I32, name="all_words", align_bytes=64)
         first_col = [(PASSES - 1 - o) * T for o in range(PASSES)]
-        xs = keep.tile([P, T], U8, name="xs", align_bytes=64)
+        xs = keep.tile([P, 2 * EARLY], U8, name="xs", align_bytes=64)
         rows = keep.tile([P, T], U8, name="rows", align_bytes=64)
         late_scales = keep.tile([P, LATE], U8, name="late_scales", align_bytes=64)
         bias = keep.tile([P, E + 1], F32, name="bias")
@@ -72,8 +73,9 @@ def tile_moe_shr_lin_bias_kernel(tc, x_words, x_scales, w, b, gate, offs, pos1, 
         nc.gpsimd.memset(rows[0:row0, :].bitcast(I32), 0)
         make_identity(nc, ident[:])
         nc.gpsimd.memset(gate_rows[:], 0.0)
+        nc.gpsimd.memset(xs[:, T:].bitcast(I32), 0)
         nc.vector.memset(rows[96:P, :].bitcast(I32), 0)
-        nc.vector.memset(xs[:].bitcast(I32), 0)
+        nc.vector.memset(xs[:, 0:T].bitcast(I32), 0)
         nc.vector.memset(xw(0, T, WINDOW), 0)
         nc.vector.memset(late_scales[:].bitcast(I32), 0)
 
@@ -85,7 +87,7 @@ def tile_moe_shr_lin_bias_kernel(tc, x_words, x_scales, w, b, gate, offs, pos1, 
         load_w(order[1])
         for q in range(4):
             nc.sync.dma_start(
-                out=xs[32 * q : 32 * q + 4 * PASSES, :].bitcast(I32),
+                out=xs[32 * q : 32 * q + 4 * PASSES, 0:T].bitcast(I32),
                 in_=x_scales[:, 4 * q : 4 * q + 4, :].bitcast(I32),
             )
         nc.sync.dma_start(out=gate_rows[0:TURNED, :], in_=gate[1, 0, 0 : TURNED * P].rearrange("(c t) -> c t", t=P))
@@ -142,8 +144,7 @@ def tile_moe_shr_lin_bias_kernel(tc, x_words, x_scales, w, b, gate, offs, pos1, 
         halves = ((0, S // 2), (S // 2, S))
         for lo, hi in halves:
             gather(gw[0][:, lo:hi], xw(0, 0, WINDOW).bitcast(U32), lo, hi)
-        for lo in range(0, EARLY, LATE):
-            gather(gs[:, lo : lo + LATE], xs[:], lo, lo + LATE)
+        gather(gs[:], xs[:], 0, EARLY)
         for e in order:
             rounded, loaded = interleaved(e)
             nc.scalar.copy(out=rounded, in_=loaded)
@@ -182,12 +183,12 @@ def tile_moe_shr_lin_bias_kernel(tc, x_words, x_scales, w, b, gate, offs, pos1, 
         for c in range(T // BANK):
             nc.scalar.copy(out=shared[:, c * BANK : (c + 1) * BANK], in_=shared_sums[c][:])
 
-        edges = (0, 512, 768, 1024, 1280, 1536)
+        spans = ((0, 512), (1152, 1536), (512, 768), (768, 1024), (1024, 1152))
         sum_banks = (0, 1, 2, 7, 3)
         totals = {}
 
         def open_total(c):
-            lo, hi = edges[c], edges[c + 1]
+            lo, hi = spans[c]
             totals[c] = psum.tile([P, hi - lo], F32, name="total%d" % c, tag="bank%d" % sum_banks[c])
             for at in range(lo, hi, P):
                 nc.tensor.matmul(
@@ -239,60 +240,51 @@ def tile_moe_shr_lin_bias_kernel(tc, x_words, x_scales, w, b, gate, offs, pos1, 
         for c in (3, 4):
             open_total(c)
 
-        units = [(lo, min(lo + UNIT, TURNED * P)) for lo in range(0, TURNED * P, UNIT)]
-        second = keep.tile([P, 2 * UNIT], F32, name="second", tag="raw1", align_bytes=64)
+        units = [
+            (c, at, min(at + UNIT, hi)) for c, (lo, hi) in enumerate(spans) for at in range(lo, min(hi, TURNED * P), UNIT)
+        ]
+        second = keep.tile([P, (AHEAD + 1) * UNIT], F32, name="second", tag="raw1", align_bytes=64)
         gated = keep.tile([P, TURNED * P], F32, name="gated", tag="raw2", align_bytes=64)
-        first = keep.tile([P, T - UNIT], F32, name="first", tag="raw3", align_bytes=64)
+        first = keep.tile([P, T], F32, name="first", tag="raw3", align_bytes=64)
         rest_second = keep.tile([P, rest], F32, name="rest_second", tag="raw4", align_bytes=64)
         res = keep.tile([P, T], F32, name="res", tag="raw5", align_bytes=64)
         forward = {}
 
         def fetch_second(u):
-            lo, hi = units[u]
-            picked = second[:, (u % 2) * UNIT : (u % 2) * UNIT + hi - lo]
+            lo, hi = units[u][1:]
+            picked = second[:, (u % (AHEAD + 1)) * UNIT : (u % (AHEAD + 1)) * UNIT + hi - lo]
             nc.scalar.activation(picked, y[:].indirect(pos_sb[1][:, lo // 16 : hi // 16]), COPY)
             forward[u] = psum.tile([P, hi - lo], F32, name="forward%d" % u, tag="bank%d" % (6 - u % 3))
             for at in range(0, hi - lo, P):
                 nc.tensor.transpose(forward[u][:, at : at + P], picked[:, at : at + P], ident[:])
 
         def gate_second(u):
-            lo, hi = units[u]
+            c, lo, hi = units[u]
             for at in range(lo, hi, P):
                 nc.scalar.activation(
                     out=gated[:, at : at + P], in_=forward[u][:, at - lo : at - lo + P], func=COPY,
                     scale=gate_cols[:, at // P : at // P + 1],
                 )
-            c = max(k for k in range(len(edges) - 1) if edges[k] <= lo)
             for at in range(lo, hi, P):
                 nc.tensor.matmul(
-                    totals[c][:, at - edges[c] : at - edges[c] + P], gated[:, at : at + P], ident[:],
-                    is_transpose=True, start=False, stop=(at + P == min(edges[c + 1], TURNED * P)),
+                    totals[c][:, at - spans[c][0] : at - spans[c][0] + P], gated[:, at : at + P], ident[:],
+                    is_transpose=True, start=False, stop=(at + P == min(spans[c][1], TURNED * P)),
                 )
 
-        fetch_second(0)
-        for u in range(1, len(units)):
-            fetch_second(u)
-            gate_second(u - 1)
-        gate_second(len(units) - 1)
-
-        def firsts(lo, hi):
-            at = lo % (T - UNIT)
-            return first[:, at : at + hi - lo]
-
-        def fetch_first(lo, hi):
-            nc.vector.tensor_tensor(firsts(lo, hi), y[:].indirect(pos_sb[0][:, lo // 16 : hi // 16]), gates[:, lo:hi], MULT)
+        for u in range(len(units) + AHEAD):
+            if u < len(units):
+                fetch_second(u)
+            if u >= AHEAD:
+                gate_second(u - AHEAD)
 
         def finish(c):
-            lo, hi = edges[c], edges[c + 1]
-            nc.vector.scalar_tensor_tensor(res[:, lo:hi], totals[c][:], bias[:, E : E + 1], firsts(lo, hi), ADD, ADD)
+            lo, hi = spans[c]
+            nc.vector.scalar_tensor_tensor(res[:, lo:hi], totals[c][:], bias[:, E : E + 1], first[:, lo:hi], ADD, ADD)
             nc.sync.dma_start(out=out[:, lo:hi], in_=res[:, lo:hi])
 
-        fetch_first(edges[0], edges[1])
-        fetch_first(edges[1], edges[4])
         nc.vector.tensor_tensor(rest_second[:], y[:].indirect(pos_sb[1][:, TURNED * P // 16 : T // 16]), rest_gates[:], MULT)
+        nc.vector.tensor_tensor(first[:], y[:].indirect(pos_sb[0][:]), gates[:], MULT)
         finish(0)
-        fetch_first(edges[4], edges[5])
-        finish(1)
-        nc.vector.tensor_tensor(firsts(T - rest, T), firsts(T - rest, T), rest_second[:], ADD)
-        for c in (2, 3, 4):
+        nc.vector.tensor_tensor(first[:, T - rest : T], first[:, T - rest : T], rest_second[:], ADD)
+        for c in range(1, len(spans)):
             finish(c)

@@ -43,9 +43,6 @@ def tile_moe_shr_lin_bias_kernel(tc, x_words, x_scales, w, b, gate, offs, pos1, 
         pos_sb = [keep.tile([P, T // 16], U16, name="pos%d" % i) for i in range(2)]
         all_words = keep.tile([P, (PASSES - 1) * T + WINDOW], I32, name="all_words", align_bytes=64)
         first_col = [(PASSES - 1 - o) * T for o in range(PASSES)]
-        xs = keep.tile([P, 2 * EARLY], U8, name="xs", align_bytes=64)
-        rows = keep.tile([P, T], U8, name="rows", align_bytes=64)
-        late_scales = keep.tile([P, LATE], U8, name="late_scales", align_bytes=64)
         bias = keep.tile([P, E + 1], F32, name="bias")
         ident = keep.tile([P, P], F32, name="ident")
         gate_rows = keep.tile([P, P], F32, name="gate_rows")
@@ -59,6 +56,9 @@ def tile_moe_shr_lin_bias_kernel(tc, x_words, x_scales, w, b, gate, offs, pos1, 
         third_raw = last_raw + 2 * RAW
         raw[E - 3] = lap.tile([P, PASSES, 4, N], F32, name="raw_third_last", offset=third_raw, align_bytes=64)
 
+        xs_at = third_raw + RAW
+        xs = lap.tile([P, 2 * EARLY], U8, name="xs", offset=xs_at, align_bytes=64)
+
         def xw(o, lo, hi):
             return all_words[:, first_col[o] + lo : first_col[o] + hi]
 
@@ -69,15 +69,15 @@ def tile_moe_shr_lin_bias_kernel(tc, x_words, x_scales, w, b, gate, offs, pos1, 
             nc.sync.dma_start(out=xw(o, 0, T), in_=x_words[o].rearrange("p t r -> p (t r)").bitcast(I32))
 
         row0 = 48
+        rows = xs[:, T : 2 * T]
         all_rows = x_scales.rearrange("o f t -> (o f) t").bitcast(I32)
         nc.gpsimd.memset(rows[0:row0, :].bitcast(I32), 0)
+        nc.gpsimd.memset(xs[:, 0:T].bitcast(I32), 0)
         make_identity(nc, ident[:])
         nc.gpsimd.memset(gate_rows[:], 0.0)
-        nc.gpsimd.memset(xs[:, T:].bitcast(I32), 0)
+        nc.gpsimd.memset(xs[:, 2 * T :].bitcast(I32), 0)
         nc.vector.memset(rows[96:P, :].bitcast(I32), 0)
-        nc.vector.memset(xs[:, 0:T].bitcast(I32), 0)
         nc.vector.memset(xw(0, T, WINDOW), 0)
-        nc.vector.memset(late_scales[:].bitcast(I32), 0)
 
         nc.sync.dma_start(offs_sb[:], offs)
         nc.sync.dma_start(out=rows[64:96, :].bitcast(I32), in_=all_rows[16:48])
@@ -128,19 +128,7 @@ def tile_moe_shr_lin_bias_kernel(tc, x_words, x_scales, w, b, gate, offs, pos1, 
         gs = keep.tile([P, EARLY], U8, name="gs", align_bytes=64)
         gw = [keep.tile([P, S if o < PASSES - 1 else EARLY], U32, name="gw%d" % o, align_bytes=64) for o in range(PASSES)]
 
-        gather(grows[:], rows[:], EARLY, S)
-        for o in range(PASSES):
-            for j in range(4):
-                nc.sync.dma_start(
-                    out=late_scales[4 * o + j : P : 32, :].bitcast(I32),
-                    in_=grows[row0 + 16 * o + j : row0 + 16 * o + 16 : 4, :].bitcast(I32),
-                )
-        rest = T - TURNED * P
-        gates = keep.tile([P, T], F32, name="gates", tag="raw0", align_bytes=64)
-        rest_gates = keep.tile([P, rest], F32, name="rest_gates", align_bytes=64)
-        nc.sync.dma_start(rest_gates[:], gate[1, :, TURNED * P : T])
-        nc.sync.dma_start(gates[:], gate[0])
-
+        gather(grows[:], rows, EARLY, S)
         halves = ((0, S // 2), (S // 2, S))
         for lo, hi in halves:
             gather(gw[0][:, lo:hi], xw(0, 0, WINDOW).bitcast(U32), lo, hi)
@@ -179,6 +167,19 @@ def tile_moe_shr_lin_bias_kernel(tc, x_words, x_scales, w, b, gate, offs, pos1, 
                     start=(o == 0 and lo % BANK == 0),
                     stop=(o == PASSES - 1 and lo % BANK == BANK - P),
                 )
+        late_scales = lap.tile([P, LATE], U8, name="late_scales", offset=xs_at + T, align_bytes=64)
+        for o in range(PASSES):
+            for j in range(4):
+                nc.sync.dma_start(
+                    out=late_scales[4 * o + j : P : 32, :].bitcast(I32),
+                    in_=grows[row0 + 16 * o + j : row0 + 16 * o + 16 : 4, :].bitcast(I32),
+                )
+        rest = T - TURNED * P
+        gates = keep.tile([P, T], F32, name="gates", tag="raw0", align_bytes=64)
+        rest_gates = keep.tile([P, rest], F32, name="rest_gates", align_bytes=64)
+        nc.sync.dma_start(rest_gates[:], gate[1, :, TURNED * P : T])
+        nc.sync.dma_start(gates[:], gate[0])
+
         shared = keep.tile([P, T], F32, name="shared", tag="raw%d" % E, align_bytes=64)
         for c in range(T // BANK):
             nc.scalar.copy(out=shared[:, c * BANK : (c + 1) * BANK], in_=shared_sums[c][:])

from contextlib import ExitStack

import concourse.mybir as mybir
from concourse.masks import make_identity

K, T, E, C, N = 1536, 1536, 12, 256, 128
S = E * C
FLOPS = 2 * K * N * (S + T)

F32 = mybir.dt.float32
BF16 = mybir.dt.bfloat16
I32 = mybir.dt.int32
U32 = mybir.dt.uint32
U16 = mybir.dt.uint16
U8 = mybir.dt.uint8
FP8X4 = mybir.dt.float8_e4m3fn_x4
MULT = mybir.AluOpType.mult
ADD = mybir.AluOpType.add
IDENT = mybir.ActivationFunctionType.Identity
COPY = mybir.ActivationFunctionType.Copy

P = 128
PASSES = 3
BANK = 512
WINDOW = 2048
LATE = 4 * C
EARLY = S - LATE
WORDS = PASSES * N
RAW = 4 * 4 * WORDS
TURNED = 11
UNIT = 256
AHEAD = 2


def tile_moe_shr_lin_bias_kernel(tc, x_words, x_scales, w, b, gate, offs, pos1, pos2, out):
    nc = tc.nc
    with ExitStack() as ctx:
        keep = ctx.enter_context(tc.tile_pool(name="keep", bufs=1))
        lap = ctx.enter_context(tc.tile_pool(name="lap", bufs=1))
        psum = ctx.enter_context(tc.psum_pool(name="psum", bufs=1))

        offs_sb = keep.tile([P, S // 16], U16, name="offs_sb")
        pos_sb = [keep.tile([P, T // 16], U16, name="pos%d" % i) for i in range(2)]
        all_words = keep.tile([P, (PASSES - 1) * T + WINDOW], I32, name="all_words", align_bytes=64)
        first_col = [(PASSES - 1 - o) * T for o in range(PASSES)]
        bias = keep.tile([P, E + 1], F32, name="bias")
        ident = keep.tile([P, P], F32, name="ident")
        gate_rows = keep.tile([P, P], F32, name="gate_rows")
        gate_cols = keep.tile([P, TURNED], F32, name="gate_cols")

        order = [E] + list(range(E))
        raw = {e: keep.tile([P, PASSES, 4, N], F32, name="raw%d" % e, align_bytes=64) for e in order[:-3]}
        last_raw = 4 * S - 2048
        raw[E - 1] = lap.tile([P, PASSES, 4, N], F32, name="raw_last", offset=last_raw, align_bytes=64)
        raw[E - 2] = lap.tile([P, PASSES, 4, N], F32, name="raw_before_last", offset=last_raw + RAW, align_bytes=64)
        third_raw = last_raw + 2 * RAW
        raw[E - 3] = lap.tile([P, PASSES, 4, N], F32, name="raw_third_last", offset=third_raw, align_bytes=64)

        xs_at = third_raw + RAW
        xs = lap.tile([P, 2 * EARLY], U8, name="xs", offset=xs_at, align_bytes=64)

        def xw(o, lo, hi):
            return all_words[:, first_col[o] + lo : first_col[o] + hi]

        def load_w(e):
            nc.sync.dma_start(out=raw[e][:], in_=w[e].rearrange("(o p r) n -> p o r n", o=PASSES, r=4))

        def load_x(o):
            nc.sync.dma_start(out=xw(o, 0, T), in_=x_words[o].rearrange("p t r -> p (t r)").bitcast(I32))

        row0 = 48
        rows = xs[:, T : 2 * T]
        all_rows = x_scales.rearrange("o f t -> (o f) t").bitcast(I32)
        nc.gpsimd.memset(rows[0:row0, :].bitcast(I32), 0)
        nc.gpsimd.memset(xs[:, 0:T].bitcast(I32), 0)
        make_identity(nc, ident[:])
        nc.gpsimd.memset(gate_rows[:], 0.0)
        nc.gpsimd.memset(xs[:, 2 * T :].bitcast(I32), 0)
        nc.vector.memset(rows[96:P, :].bitcast(I32), 0)
        nc.vector.memset(xw(0, T, WINDOW), 0)

        nc.sync.dma_start(offs_sb[:], offs)
        nc.sync.dma_start(out=rows[64:96, :].bitcast(I32), in_=all_rows[16:48])
        nc.sync.dma_start(out=rows[row0:64, :].bitcast(I32), in_=all_rows[0:16])
        load_x(0)
        load_w(order[0])
        load_w(order[1])
        for q in range(4):
            nc.sync.dma_start(
                out=xs[32 * q : 32 * q + 4 * PASSES, 0:T].bitcast(I32),
                in_=x_scales[:, 4 * q : 4 * q + 4, :].bitcast(I32),
            )
        nc.sync.dma_start(out=gate_rows[0:TURNED, :], in_=gate[1, 0, 0 : TURNED * P].rearrange("(c t) -> c t", t=P))
        nc.sync.dma_start(bias[:], b)
        for e in order[2:5]:
            load_w(e)
        load_x(1)
        nc.sync.dma_start(pos_sb[0][:], pos1)
        nc.sync.dma_start(pos_sb[1][:], pos2)
        for e in order[5:10]:
            load_w(e)
        load_x(2)
        for e in order[10:]:
            load_w(e)

        stage = keep.tile([P, 4 * (E + 1) * WORDS], BF16, name="stage", align_bytes=64)
        codes = keep.tile([P, (E + 1) * WORDS], U32, name="codes", align_bytes=64)
        scales = keep.tile([P, (E + 1) * WORDS], U8, name="scales", align_bytes=64)

        def matrix(tile, e, o):
            at = order.index(e) * WORDS + o * N
            return tile[:, at : at + N]

        def interleaved(e):
            at = 4 * order.index(e) * WORDS
            return (
                stage[:, at : at + 4 * WORDS].rearrange("p (o c i r) -> p o c r i", o=PASSES, i=4, r=4),
                raw[e][:].rearrange("p o r (c i) -> p o c r i", i=4),
            )

        def quantize(lo, hi):
            nc.vector.quantize_mx(out=codes[:, lo:hi].bitcast(FP8X4), scales=scales[:, lo:hi], in_=stage[:, 4 * lo : 4 * hi])

        def gather(dst, window, lo, hi):
            nc.vector.tensor_copy(dst, window.indirect(offs_sb[:, lo // 16 : hi // 16]))

        grows = keep.tile([P, LATE], U8, name="grows", align_bytes=64)
        gs = keep.tile([P, EARLY], U8, name="gs", align_bytes=64)
        gw = [keep.tile([P, S if o < PASSES - 1 else EARLY], U32, name="gw%d" % o, align_bytes=64) for o in range(PASSES)]

        gather(grows[:], rows, EARLY, S)
        halves = ((0, S // 2), (S // 2, S))
        for lo, hi in halves:
            gather(gw[0][:, lo:hi], xw(0, 0, WINDOW).bitcast(U32), lo, hi)
        gather(gs[:], xs[:], 0, EARLY)
        for e in order:
            rounded, loaded = interleaved(e)
            nc.scalar.copy(out=rounded, in_=loaded)
        quantize(0, 1024)
        for lo, hi in halves:
            gather(gw[1][:, lo:hi], xw(1, 0, WINDOW).bitcast(U32), lo, hi)
        quantize(1024, 2048)
        quantize(2048, 3072)
        gather(gw[2][:], xw(2, 0, 2 * WINDOW).bitcast(U32), 0, EARLY)
        quantize(3072, 4096)
        next_words = lap.tile([P, 2 * C], U32, name="next_words", offset=third_raw, align_bytes=64)
        gather(next_words[:], xw(2, 0, T).bitcast(U32), EARLY, EARLY + 2 * C)
        quantize(4096, 4608)
        quantize(4608, 4992)
        last_words = lap.tile([P, 2 * C], U32, name="last_words", offset=last_raw + RAW - 4 * C, align_bytes=64)
        for lo in (0, C):
            gather(last_words[:, lo : lo + C], xw(2, 0, T).bitcast(U32), S - 2 * C + lo, S - C + lo)

        turned_gates = psum.tile([P, P], F32, name="turned_gates", tag="bank7")
        nc.tensor.transpose(turned_gates[:], gate_rows[:], ident[:])
        nc.scalar.copy(out=gate_cols[:], in_=turned_gates[:, 0:TURNED])

        shared_sums = [psum.tile([P, BANK], F32, name="shared%d" % c, tag="bank%d" % (4 + c)) for c in range(T // BANK)]
        for o in range(PASSES):
            for lo in range(0, T, P):
                nc.tensor.matmul_mx(
                    out=shared_sums[lo // BANK][:, lo % BANK : lo % BANK + P],
                    lhsT=xw(o, lo, lo + P).bitcast(FP8X4),
                    lhsT_scale=xs[4 * o : P, lo : lo + P],
                    rhs=matrix(codes, E, o).bitcast(FP8X4),
                    rhs_scale=matrix(scales, E, o),
                    start=(o == 0 and lo % BANK == 0),
                    stop=(o == PASSES - 1 and lo % BANK == BANK - P),
                )
        late_scales = lap.tile([P, LATE], U8, name="late_scales", offset=xs_at + T, align_bytes=64)
        for o in range(PASSES):
            for j in range(4):
                nc.sync.dma_start(
                    out=late_scales[4 * o + j : P : 32, :].bitcast(I32),
                    in_=grows[row0 + 16 * o + j : row0 + 16 * o + 16 : 4, :].bitcast(I32),
                )
        rest = T - TURNED * P
        gates = keep.tile([P, T], F32, name="gates", tag="raw0", align_bytes=64)
        rest_gates = keep.tile([P, rest], F32, name="rest_gates", align_bytes=64)
        nc.sync.dma_start(rest_gates[:], gate[1, :, TURNED * P : T])
        nc.sync.dma_start(gates[:], gate[0])

        shared = keep.tile([P, T], F32, name="shared", tag="raw%d" % E, align_bytes=64)
        for c in range(T // BANK):
            nc.scalar.copy(out=shared[:, c * BANK : (c + 1) * BANK], in_=shared_sums[c][:])

        spans = ((0, 512), (1152, 1536), (512, 768), (768, 1024), (1024, 1152))
        sum_banks = (0, 1, 2, 7, 3)
        totals = {}

        def open_total(c):
            lo, hi = spans[c]
            totals[c] = psum.tile([P, hi - lo], F32, name="total%d" % c, tag="bank%d" % sum_banks[c])
            for at in range(lo, hi, P):
                nc.tensor.matmul(
                    totals[c][:, at - lo : at - lo + P], shared[:, at : at + P], ident[:],
                    is_transpose=True, start=(at == lo), stop=False,
                )

        for c in range(3):
            open_total(c)

        def product(acc, o, lo, hi, start, stop):
            e = lo // C
            if o < PASSES - 1 or lo < EARLY:
                words = gw[o][:, lo:hi]
            elif lo < S - 2 * C:
                words = next_words[:, lo - EARLY : hi - EARLY]
            else:
                words = last_words[:, lo - (S - 2 * C) : hi - (S - 2 * C)]
            nc.tensor.matmul_mx(
                out=acc,
                lhsT=matrix(codes, e, o).bitcast(FP8X4),
                lhsT_scale=matrix(scales, e, o),
                rhs=words.bitcast(FP8X4),
                rhs_scale=late_scales[4 * o : P, lo - EARLY : hi - EARLY] if lo >= EARLY else gs[4 * o : P, lo:hi],
                start=start,
                stop=stop,
            )

        y = lap.tile([P, S], F32, name="y", offset=0, align_bytes=64)

        def empty(acc, lo, hi):
            e = lo // C
            nc.scalar.activation(out=y[:, lo:hi], in_=acc, func=IDENT, bias=bias[:, e : e + 1])

        pairs = [psum.tile([P, 2, C], F32, name="pair%d" % h, tag="bank%d" % (3 + h)) for h in range(E // 2 - 1)]
        for first, end in ((0, 4), (4, 5)):
            for o in range(PASSES):
                for e in range(2 * first, 2 * end):
                    product(pairs[e // 2][:, e % 2, :], o, e * C, (e + 1) * C, o == 0 and e % 2 == 0, o == PASSES - 1 and e % 2 == 1)
            for e in range(2 * first, 2 * end):
                empty(pairs[e // 2][:, e % 2, :], e * C, (e + 1) * C)
        ends = ((S - 2 * C, S - C), (S - C, S - P), (S - P, S))
        lone = [psum.tile([P, hi - lo], F32, name="lone%d" % j, tag="bank%d" % (3 + j)) for j, (lo, hi) in enumerate(ends)]
        for o in range(PASSES):
            for j, (lo, hi) in enumerate(ends):
                product(lone[j][:], o, lo, hi, o == 0, o == PASSES - 1)
        for j, (lo, hi) in enumerate(ends):
            empty(lone[j][:], lo, hi)
        for c in (3, 4):
            open_total(c)

        units = [
            (c, at, min(at + UNIT, hi)) for c, (lo, hi) in enumerate(spans) for at in range(lo, min(hi, TURNED * P), UNIT)
        ]
        second = keep.tile([P, (AHEAD + 1) * UNIT], F32, name="second", tag="raw1", align_bytes=64)
        gated = keep.tile([P, TURNED * P], F32, name="gated", tag="raw2", align_bytes=64)
        first = keep.tile([P, T], F32, name="first", tag="raw3", align_bytes=64)
        rest_second = keep.tile([P, rest], F32, name="rest_second", tag="raw4", align_bytes=64)
        res = keep.tile([P, T], F32, name="res", tag="raw5", align_bytes=64)
        forward = {}

        def fetch_second(u):
            lo, hi = units[u][1:]
            picked = second[:, (u % (AHEAD + 1)) * UNIT : (u % (AHEAD + 1)) * UNIT + hi - lo]
            nc.scalar.activation(picked, y[:].indirect(pos_sb[1][:, lo // 16 : hi // 16]), COPY)
            forward[u] = psum.tile([P, hi - lo], F32, name="forward%d" % u, tag="bank%d" % (6 - u % 3))
            for at in range(0, hi - lo, P):
                nc.tensor.transpose(forward[u][:, at : at + P], picked[:, at : at + P], ident[:])

        def gate_second(u):
            c, lo, hi = units[u]
            for at in range(lo, hi, P):
                nc.scalar.activation(
                    out=gated[:, at : at + P], in_=forward[u][:, at - lo : at - lo + P], func=COPY,
                    scale=gate_cols[:, at // P : at // P + 1],
                )
            for at in range(lo, hi, P):
                nc.tensor.matmul(
                    totals[c][:, at - spans[c][0] : at - spans[c][0] + P], gated[:, at : at + P], ident[:],
                    is_transpose=True, start=False, stop=(at + P == min(spans[c][1], TURNED * P)),
                )

        for u in range(len(units) + AHEAD):
            if u < len(units):
                fetch_second(u)
            if u >= AHEAD:
                gate_second(u - AHEAD)

        def finish(c):
            lo, hi = spans[c]
            nc.vector.scalar_tensor_tensor(res[:, lo:hi], totals[c][:], bias[:, E : E + 1], first[:, lo:hi], ADD, ADD)
            nc.sync.dma_start(out=out[:, lo:hi], in_=res[:, lo:hi])

        nc.vector.tensor_tensor(rest_second[:], y[:].indirect(pos_sb[1][:, TURNED * P // 16 : T // 16]), rest_gates[:], MULT)
        nc.vector.tensor_tensor(first[:], y[:].indirect(pos_sb[0][:]), gates[:], MULT)
        finish(0)
        nc.vector.tensor_tensor(first[:, T - rest : T], first[:, T - rest : T], rest_second[:], ADD)
        for c in range(1, len(spans)):
            finish(c)
